import numpy as np, ml_dtypes
CORES = [1,5,17,21,33,37,49,53]
N = 8
import mx_ref
BF = ml_dtypes.bfloat16
def gentries(a):
    return np.ascontiguousarray(a.reshape(8, 16, -1).transpose(0, 2, 1)).reshape(8, -1)
def gtable(e):
    e = np.asarray(e); return np.ascontiguousarray(e.reshape(8, -1, 16).transpose(0, 2, 1)).reshape(128, -1).astype(np.int32)
def gcols(t, e):
    v = np.concatenate([t.reshape(8, 16, -1, 4), np.zeros((8, 16, 1, 4), BF)], axis=2)
    return np.ascontiguousarray(np.stack([v[g][:, e[g]] for g in range(8)])).reshape(128, -1)
def tile(rs):
    return np.stack(rs, axis=2).reshape(128, -1).astype(BF)
def pick(q, e):
    c = np.concatenate([q[0].reshape(128, -1, 4), np.zeros((128, 1, 4), np.uint8)], axis=1); s = np.concatenate([q[1], np.ones((16, 1), np.uint8)], axis=1)
    return (np.ascontiguousarray(c[:, e].reshape(128, -1)), np.ascontiguousarray(s[:, e]))
def join(*qs):
    return (np.concatenate([q[0] for q in qs], axis=1), np.concatenate([q[1] for q in qs], axis=1))
def put(q, e, v):
    c, s = q[0].reshape(128, -1, 4).copy(), q[1].copy(); c[:, e] = v[0].reshape(128, -1, 4); s[:, e] = v[1]
    return (c.reshape(128, -1), s)
def pk(c, s):
    return (np.ascontiguousarray(c), mx_ref.live(s))
def emit(q):
    return q[0], q[1]
def packed(v, rng):
    q = [mx_ref.quantize(np.ascontiguousarray(v[r])) for r in range(N)]
    return np.stack([a for a, b in q]), np.stack([mx_ref.plane(b, rng) for a, b in q])
def values_of_codes():
    e, c = np.zeros((128, 128, 4), np.float32), np.zeros((128, 2, 4), np.uint8)
    e[np.arange(128), np.arange(128), 0] = 1
    c[:127, :, 0] = np.arange(256).reshape(2, 128).T[:127]
    return mx_ref.matmul(mx_ref.quantize(e.reshape(128, 512).astype(BF)), (c.reshape(128, 8), np.full((16, 2), 127, np.uint8))).T.reshape(-1).astype(np.float64)
CODE_VALUE, SCALE_VALUE = values_of_codes(), 2.0 ** (np.arange(256) - 127.0)
def decode(q):
    return (CODE_VALUE[q[0]].reshape(16, 8, -1, 4) * SCALE_VALUE[q[1]][:, None, :, None] + 0.0).reshape(128, -1).astype(np.float32)
def f(rng, *shape):
    return mx_ref.flush((rng.standard_normal(shape, dtype=np.float32) * np.exp2(rng.integers(-2, 3, shape[:-1] + (1,)))).astype(BF))
def wide(rng, *shape, cols=0):
    v = rng.standard_normal(shape, dtype=np.float32) * np.exp2(rng.integers(-12, 13, shape)).astype(np.float32)
    if cols: v *= np.repeat(np.exp2(rng.integers(-cols, cols + 1, shape[:-2] + (1, shape[-1] // 4))) * (rng.random(shape[:-2] + (1, shape[-1] // 4)) > 0.0625), 4, axis=-1).astype(np.float32)
    return mx_ref.flush(v.astype(BF))
C = 320
STEP = [1, 2, 4]
def take(a, e):
    return np.take_along_axis(a, e, axis=-1)
def effective(back):
    e = np.ones(back.shape, bool)
    for j in range(C - 1, -1, -1):
        up = back[..., j]
        e[..., j] = (up <= j) | ~take(e, up[..., None])[..., 0]
    return e
def numbers_of(rng):
    return {"x": np.array(f(rng, N, 128, 4 * C)), "u": np.array(f(rng, N, 128, 512)), "v": np.array(f(rng, N, 128, 512))}
def stored(back, ring, mate):
    return {k: np.stack([gtable(e[r]) for r in range(N)]) for k, e in (("ud", np.argsort(back, axis=-1)), ("iv", back), ("hp", ring), ("mt", mate))}
def shuffled(rng):
    return rng.permuted(np.tile(np.arange(C), (N, 8, 1)), axis=2)
def linked(order):
    e = np.zeros_like(order)
    np.put_along_axis(e, order, np.roll(order, -1, axis=-1), axis=-1)
    return e
def mates(rng):
    a = shuffled(rng)
    e = np.zeros_like(a)
    np.put_along_axis(e, a[..., ::2], a[..., 1::2], axis=-1)
    np.put_along_axis(e, a[..., 1::2], a[..., ::2], axis=-1)
    return e
def runs(rng, back):
    return linked(np.argsort(effective(back) + rng.random(back.shape), axis=-1))
def lists(rng):
    return stored(shuffled(rng), linked(shuffled(rng)), mates(rng))
def layers(rng, still=()):
    w = np.array(f(rng, N, 128, 2048)).reshape(N, 8, 16, 4, 8, 16, 4)
    for i in still:
        w[:, :, i] = 0
        w[:, :, :, :, :, i] = 0
    return w
def weights(rng, w):
    c, s = packed(np.ascontiguousarray(w).reshape(N, 128, 2048), rng)
    return {"wc": c, "ws": s}
def setup_inputs(rng):
    return {**numbers_of(rng), **lists(rng), **weights(rng, layers(rng))}
def setup_inputs_ties(rng):
    d = numbers_of(rng)
    o = rng.permutation(N)
    k = rng.choice([-1.0, 0.0, 1.0, 1.0], (N, 8, C))
    k[o[0]] = 0
    k[o[1]] = 1
    k[o[2]] = (rng.permutation(8) % 2 * 2.0 - 1.0)[:, None]
    x = d["x"].reshape(N, 8, 16, C, 4)
    x[:, :, 0] = 0
    x[:, :, 0, :, 0] = k.astype(np.float32).astype(BF)
    u = d["u"].reshape(N, 128, 128, 4)
    u[:, :, ::16] = 0
    for h in range(0, 128, 16): u[:, h, h, 0] = 1
    back = np.zeros((N, 8, C), np.int64)
    for r in range(N):
        for g, m in enumerate(rng.permutation([1, 1, 1, 2, 2, 3, C // 8, 0])):
            a = rng.integers(0, m, C) if m else np.arange(C)
            for i in np.unique(a):
                e = np.flatnonzero(a == i)
                back[r, g, e] = np.roll(e, -1)
    mate = mates(rng)
    tau = np.where((k > 0) & (take(k, mate) > 0), mate, np.arange(C))
    return {"x": x.reshape(N, 128, 4 * C), "u": u.reshape(N, 128, 512), "v": d["v"], **stored(take(tau, back), runs(rng, back), mate), **weights(rng, layers(rng, [0]))}
def setup_inputs_near(rng):
    d = numbers_of(rng)
    i = np.arange(N)
    first = np.minimum(i, i ^ STEP[0])
    small = np.isin(first, rng.permutation(np.unique(first))[:N // 4])
    k = np.where(small, 2.0 ** -30, 1.0)
    x = d["x"].astype(np.float32).reshape(N, 8, 16, C, 4)
    x[:, :, :8] = 0
    s = rng.choice([-1.0, 0.0, 1.0, 1.0], (N, 8, C)) * k[:, None, None]
    x[:, :, 0, :, 0] = 1.125 * s
    x[:, :, 1, :, 0] = -1.25 * s
    x[:, :, 3, :, 0] = np.where(small[:, None, None], rng.choice([-1.0, 1.0], (N, 8, C)) * 2.0 ** -30, 0.0)
    x[:, :, 4, :, 0] = np.where(small, 2.0 ** -27, 0.0)[:, None, None]
    u = d["u"].reshape(N, 128, 128, 4)
    u[:, :, ::16] = 0
    w = layers(rng, range(8))
    for r in range(N):
        at = [0, C - 1, int(rng.integers(C)), int(rng.integers(C))]
        for g, j in zip(rng.permutation(8)[:4], at): x[r, g, 0, j, 0] = 2.0 ** 30 * rng.choice([-1.0, 1.0])
        for g in range(8):
            h = 16 * g
            u[r, h, h, 0] = 1.125 * k[r]
            u[r, h + 1, h, 0] = k[r]
            u[r, h + 2, h, 0] = 1.125 * k[r]
            u[r, h + 5, h, 0] = k[r]
            if small[r]:
                w[r, g, 3, 0, g, 2, 0] = 2.0 ** -7
                w[r, g, 3, 0, g, 5, 0] = -2.0 ** -7
    return {"x": x.reshape(N, 128, 4 * C).astype(BF), "u": u.reshape(N, 128, 512), "v": d["v"], **lists(rng), **weights(rng, w)}
def setup_inputs_odd(rng):
    d = numbers_of(rng)
    x = (1.0 + (2 * rng.integers(0, 64, (N, 16, 8, C, 4)) + 1) * 2.0 ** -7) * np.exp2(-rng.integers(0, 7, (N, 16, 8, C, 4)).astype(np.float64)) * rng.choice([-1.0, 1.0], (N, 16, 8, C, 4))
    x[:, ::2] = 0
    x[:, :, 0, :, 0] = 1.96875 * 2.0 ** 8 * rng.choice([-1.0, 1.0], (N, 16, C))
    x[:, ::2, 1, :, 0] = (1.0 + 0.125 * (rng.random((N, 8, C)) < 0.75)) * 2.0 ** -5
    x[:, ::2, 2, :, 0] = (1.0 + 0.125 * (rng.random((N, 8, C)) < 0.25)) * 2.0 ** -5
    x[:, 14, 0, :, 1] = 16.0
    u = d["u"].reshape(N, 128, 128, 4)
    u[:, :, ::16] = 0
    for h in range(0, 128, 16):
        u[:, h + 1, h, 0] = 1
        u[:, h + 2, h, 0] = -1
        u[:, h + 3, h, 0] = 1
    w = layers(rng, [0, 1, 2, 8])
    w[:, 7, 0, 0, :, 0, 1] = -16.0
    return {"x": x.astype(np.float32).reshape(N, 128, 4 * C).astype(BF), "u": u.reshape(N, 128, 512), "v": d["v"], **lists(rng), **weights(rng, w)}
def setup_inputs_ends(rng):
    d = numbers_of(rng)
    x = np.zeros((N, 8, 16, C, 4))
    u = d["u"].astype(np.float32).reshape(N, 128, 128, 4)
    v = d["v"].astype(np.float32)
    w = np.zeros((N, 128, 4, 128, 4), np.float32)
    o, kinds = np.zeros(N, np.int64), rng.permutation(4)
    left = rng.permutation(np.unique(np.minimum(np.arange(N), np.arange(N) ^ STEP[0])))
    o[left] = kinds[:N // 2]
    o[left ^ STEP[0]] = kinds[(np.arange(N // 2) + 2) % 4]
    i, j = np.arange(128), np.arange(C)
    turns = np.stack([j ^ 1, C - 1 - j, (j + C // 2) % C])
    ways = np.stack([np.roll(j, -1), j, C - 1 - j, np.roll(j, 1)])
    mate = np.stack([turns[rng.permutation(8) % 3] for r in range(N)])
    plan = np.stack([ways[rng.permutation(8) % 4] for r in range(N)])
    ring, back = runs(rng, plan), plan.copy()
    for r in range(N):
        h = rng.permutation(8)
        sign = np.where(h < 2, 0.0, h % 2 * 2.0 - 1.0)
        c = sign[None, :, None]
        e = rng.permutation(8)
        ring[r, e[:2]] = np.roll(j, -1)
        ring[r, e[2:4]] = np.roll(j, 1)
        if o[r] in (0, 2): back[r, sign < 0] = take(mate[r], plan[r])[sign < 0]
        low = -(0.9 + 0.1 * rng.random((8, 16, C, 4))) * 2.0 ** 30
        if o[r] == 0: x[r] = low
        if o[r] == 1: x[r] = np.where((rng.random(C) < 0.5)[:, None], (1.0 + 0.4 * rng.random((8, 16, C, 4))) * 2.0 ** 27, low)
        if o[r] == 2: x[r] = -(1.0 + 0.125 * rng.integers(0, 8, (8, 16, C, 4))) * 2.0 ** -30
        if o[r] == 3: x[r] = d["x"][r].astype(np.float32).reshape(8, 16, C, 4)[:, :, :1]
        if o[r] < 2:
            x[r, 7, 15, :, 3] *= 2.0 ** -6
            u[r, :, ::16] = c * (0.9 + 0.1 * rng.random((128, 8, 4))) * 2.0 ** 30
            v[r] = rng.choice([-1.0, 1.0], (128, 512)) * (0.9 + 0.1 * rng.random((128, 512))) * 2.0 ** 30
        if o[r] == 2:
            u[r, :, ::16] = c * (1.0 + 0.125 * rng.integers(0, 8, (128, 8, 4))) * 2.0 ** -30
            v[r] = rng.choice([-1.0, 1.0], (128, 512)) * (1.0 + 0.125 * rng.integers(0, 8, (128, 512))) * 2.0 ** -30
        if o[r] == 3: u[r, :, ::16] *= np.abs(c).astype(np.float32)
        k = np.array([8.0, 16.0, 32.0])[rng.permutation(8) % 3]
        for b in range(4): w[r, i, b, i, b] = k[i // 16]
        if o[r] == 2:
            w[r, 127, 3, 127, 3] = 256.0
            w[r, 126, 3, 126, 3] = 2.0 ** -8
    return {"x": x.astype(np.float32).reshape(N, 128, 4 * C).astype(BF), "u": u.reshape(N, 128, 512).astype(BF), "v": v.astype(BF), **stored(back, ring, mate), **weights(rng, w.astype(BF))}
def setup_inputs_spread(rng):
    d = setup_inputs(rng)
    d["x"] = wide(rng, N, 128, 4 * C, cols=6)
    return d
def check_inputs(d):
    b = []
    for k in ("x", "u", "v"):
        a = np.abs(d[k].astype(np.float32))
        if not (np.isfinite(a).all() and ((a == 0) | (a >= 2.0 ** -30) & (a <= 2.0 ** 30)).all()): b.append("a value of " + k)
    none, least, most = [emit(mx_ref.quantize(np.full((128, 16), k, np.float32).astype(BF)))[1][0, 0] for k in (0.0, 2.0 ** -8, 2.0 ** 8)]
    own = np.arange(C)
    for r in range(N):
        ud, iv, hp, mt = [gentries(d[k][r]) for k in ("ud", "iv", "hp", "mt")]
        if any(((a < 0) | (a >= C)).any() for a in (ud, iv, hp, mt)): b.append("an entry of a list")
        else:
            if (np.sort(ud, axis=1) != own).any(): b.append("ud: a permutation")
            if (take(ud, iv) != own).any(): b.append("iv: the inverse of ud")
            if (take(mt, mt) != own).any() or (mt == own).any(): b.append("mt: pairs of columns")
            at, seen = np.zeros((8, 1), np.int64), np.zeros((8, C), bool)
            for j in range(C):
                at = take(hp, at)
                np.put_along_axis(seen, at, True, axis=1)
            if not seen.all(): b.append("hp: a ring")
        if ((d["wc"][r] == 0x7F) | (d["wc"][r] == 0xFF)).any(): b.append("wc: a code that is no number")
        s = mx_ref.live(d["ws"][r])
        if ((s != none) & ((s < least) | (s > most))).any(): b.append("ws: a scale out of range")
    return b
def halfsum(s, t):
    return ((s.astype(np.float32) + t.astype(np.float32)) * np.float32(0.5)).astype(BF)
def reference(x, u, v, ud, iv, hp, mt, wc, ws):
    qu = [mx_ref.quantize(u[r]) for r in range(N)]
    lay = [pk(wc[r], ws[r]) for r in range(N)]
    to, back, ring, mate = [[gentries(a[r]) for r in range(N)] for a in (ud, iv, hp, mt)]
    now = [x[r] for r in range(N)]
    for step in STEP:
        t, past, sent = [], [], []
        for r in range(N):
            q = mx_ref.quantize(now[r])
            s = mx_ref.matmul(qu[r], q)[::16] > 0
            t.append(decode(q).astype(BF))
            tau = np.where(s & take(s, mate[r]), mate[r], np.arange(C))
            to[r], back[r] = take(to[r], tau), take(tau, back[r])
            e, b = effective(back[r]), ring[r]
            while not take(e, b).all(): b = np.where(take(e, b), b, take(ring[r], b))
            past.append(b)
            sent.append(mx_ref.quantize(halfsum(gcols(t[r], b), gcols(t[r], back[r]))))
        for r in range(N):
            p = r ^ step
            h = tile([mx_ref.matmul(pick(lay[r], np.arange(128 * b, 128 * b + 128)), sent[p]) * np.float32(0.03125) for b in range(4)])
            now[r] = halfsum(gcols(t[r], to[r]), gcols(h, take(past[p], back[r])))
    y, uo = np.zeros((N, 128, C), np.float32), np.zeros((N, 8, C), np.float32)
    oc, osc = np.zeros((N, 128, 4 * C), np.uint8), np.zeros((N, 16, C), np.uint8)
    for r in range(N):
        q = mx_ref.quantize(now[r])
        y[r] = mx_ref.matmul(mx_ref.quantize(v[r]), q)
        uo[r] = to[r]
        oc[r], osc[r] = emit(q)
    return {"y": y, "uo": uo, "oc": oc, "osc": osc}

@@ -1,0 +1,421 @@
+from concourse.bass import DstId, RemoteDMATransfer
+from concourse.mybir import dt, AluOpType as A, ActivationFunctionType as F
+
+C = 320
+RAD = [4, 4, 4, 5]
+SIZES = [4, 16, 64, 320]
+STEP = [1, 2, 4]
+PADZ = 16
+BIG, LOW = 1024.0, -8192.0
+BIGS, LOWS = 4.0, -64.0
+FRAC = 1.0 / 1024.0
+F4, U8, BF, F32, I32, U16 = "float8_e4m3fn_x4", "uint8", "bfloat16", "float32", "int32", "uint16"
+
+SCRATCH = {}
+SEMAPHORES = ["qv", "qs", "qt", "qg", "sent"]
+
+
+def _buf(name, n, dtype):
+    SCRATCH[name] = ("sbuf", [128, n], dtype)
+
+
+for _n in ("ud", "iv", "hp", "mt"):
+    _buf(_n + "in", 20, I32)
+    _buf(_n + "o", 20, U16)
+    SEMAPHORES.append("d" + _n)
+for _n in ("x", "u", "v", "wc", "ws", "y0", "y1", "oc", "s0", "s1", "s2", "s3", "uo"):
+    SEMAPHORES.append("d" + _n)
+for _n, _w, _t in (("xin", 1280, BF), ("uin", 512, BF), ("vin", 512, BF), ("eb", 520, BF), ("ones", 520, BF),
+                   ("iotj", C, F32), ("iotc", 328, F32), ("ti", C, I32), ("c16", 20, I32), ("pa", 2, I32),
+                   ("msk", C, F32), ("msks", C, BF),
+                   ("pf", 2, F32), ("bigc", 2, F32), ("bigs", 2, F32), ("eif", 20, F32), ("cj", 20, F32), ("kk", 80, F32),
+                   ("hpw", C, F32), ("mtw", C, F32), ("ivmw", C, F32), ("xa", C, F32), ("xb", C, F32),
+                   ("rd0", C, F32), ("rd1", C, F32), ("rdc", C, F32), ("sg", C, F32), ("rsc", C, F32), ("rt", 20, F32), ("rofs", 20, U16), ("pos", 20, F32),
+                   ("poso", 20, U16), ("peq", 20, F32), ("pmo", 20, U16), ("rw", 328, F32), ("wd", C, F32), ("ordo", 20, U16),
+                   ("da", C, F32), ("dd", C, F32), ("tt", C, F32), ("sc", C, F32), ("scs", C, BF), ("t1", 20, F32),
+                   ("ivs", 20, F32), ("ivd", 20, F32), ("uds", 20, F32), ("udd", 20, F32), ("sf", 20, F32), ("sm", 20, F32), ("sn", 20, F32),
+                   ("xle", 20, F32), ("xao", 20, U16), ("xbo", 20, U16), ("oa", 22, U16), ("ob", 22, U16),
+                   ("pp", C, BF), ("sw", C, BF), ("giv", C, BF), ("vi", C, I32), ("ne", C, F32), ("st", C, F32), ("bw", C, F32), ("ew", C, F32), ("sce", C, F32),
+                   ("th", 1280, BF), ("thp", 1280, BF), ("tiv", 1280, BF), ("tu", 1280, BF), ("hh", 1280, BF), ("xt", 1280, BF), ("zt", 1280, BF),
+                   ("uof", 8, U16), ("ys", C, F32),
+                   ("qu", 128, F4), ("su", 128, U8), ("qr", 128, F4), ("sr", 128, U8), ("qv_", 128, F4), ("sv", 128, U8),
+                   ("qw", 512, F4), ("sw_", 512, U8), ("qe", 512, F4), ("se", 512, U8), ("qz", C, F4), ("sz", C, U8), ("udn", 20, U16)):
+    _buf(_n, _w, _t)
+for _n in ("ivn", "ivp", "bn", "bp", "en", "ep"):
+    _buf(_n, 72, U16)
+for _i in range(4):
+    _buf("d%d" % _i, 16 + C, F32)
+    _buf("qx%d" % _i, C, F4)
+    _buf("sx%d" % _i, C, U8)
+for _i in range(3):
+    _buf("qp%d" % _i, C, F4)
+    _buf("sp%d" % _i, C, U8)
+    SEMAPHORES += ["%s%d" % (_n, _i) for _n in ("aq", "as", "ai", "ab", "ae")]
+for _i in range(8):
+    SCRATCH["ps%d" % _i] = ("psum", [128, 512], F32)
+
+
+def rank_program(g, core, T, topo):
+    rank = T.rank_of(core)
+    if rank is None:
+        return
+    V, S, P, Y = g.vector, g.scalar, g.tensor, g.sync
+    eng = {"v": V, "s": S, "t": P, "g": g, "y": Y}
+    count = {"qv": 0, "qs": 0, "qt": 0, "qg": 0}
+    seen = {q: {} for q in eng}
+    lastw, readers = {}, {}
+    total = {}
+
+    def need(q, rd, wr):
+        dep = {}
+        for k in rd:
+            for s, n in lastw.get(k, ()):
+                dep[s] = max(dep.get(s, 0), n)
+        for k in wr:
+            for s, n in list(lastw.get(k, ())) + readers.get(k, []):
+                dep[s] = max(dep.get(s, 0), n)
+        for s, n in dep.items():
+            if seen[q].get(s, 0) < n:
+                eng[q].wait_ge(T.sem[s], n)
+                seen[q][s] = n
+
+    def note(tok, rd, wr):
+        for k in rd:
+            readers.setdefault(k, []).append(tok)
+        for k in wr:
+            lastw[k] = [tok]
+            readers[k] = []
+
+    def op(q, name, rd, wr, *a, **kw):
+        need(q, rd, wr)
+        f = {"copy": V.tensor_copy, "tt": V.tensor_tensor, "ts": V.tensor_scalar, "scan": V.tensor_tensor_scan, "set": V.memset,
+             "quant": V.quantize_mx, "act": S.activation, "mm": P.matmul_mx, "iota": g.iota, "sel": g.affine_select}[name]
+        s = "q" + q
+        count[s] += 1
+        f(*a, **kw).then_inc(T.sem[s], 1)
+        total[s] = count[s]
+        note((s, count[s]), rd, wr)
+
+    def dma(q, sem, rd, wr, out, in_):
+        need(q, rd, wr)
+        total[sem] = total.get(sem, 0) + 16
+        eng[q].dma_start(out, in_).then_inc(T.sem[sem], 16)
+        note((sem, total[sem]), rd, wr)
+
+    def send(p, key, out, in_, sem):
+        need("g", [key], [])
+        dst = T.cores[p]
+        rid, pid = topo.addr(dst)[:2]
+        e = topo.engines(core, dst)[:8]
+        total["sent"] = total.get("sent", 0) + len(e)
+        g.remote_dma(out, in_, T.sem[sem], T.sem.sent, pid, rid, sum(1 << i for i in e))
+
+    def lands(key, sem, p):
+        n = len(topo.engines(T.cores[p], core)[:8])
+        lastw[key] = [(sem, n)]
+        total[sem] = n
+
+    for r in range(3):
+        p = rank ^ STEP[r]
+        for k, s in (("qp", "aq"), ("sp", "as"), ("ivp", "ai"), ("bp", "ab"), ("ep", "ae")):
+            lands("%s%d" % (k, r), "%s%d" % (s, r), p)
+
+    def li(name, lo=0, hi=20):
+        if name[:-1] in ("ivn", "ivp", "bn", "bp", "en", "ep"):
+            o = 24 * int(name[-1])
+            return T[name[:-1]][:, o + lo:o + hi]
+        return T[name][:, lo:hi]
+
+    dma("y", "dhp", [], ["hpin"], T.hpin[:], T.hp[:])
+    dma("s", "div", [], ["ivin"], T.ivin[:], T.iv[:])
+    dma("y", "dx", [], ["xin"], T.xin[:], T.x[:])
+    dma("s", "dmt", [], ["mtin"], T.mtin[:], T.mt[:])
+    dma("y", "du", [], ["uin"], T.uin[:], T.u[:])
+    dma("s", "dud", [], ["udin"], T.udin[:], T.ud[:])
+    dma("y", "dws", [], ["sw_"], T.sw_[:], T.ws[:])
+    dma("y", "dwc", [], ["qw"], T.qw[:].bitcast(dt.uint8), T.wc[:])
+    dma("y", "dv", [], ["vin"], T.vin[:], T.v[:])
+
+    op("g", "iota", [], ["iotj"], T.iotj[:], [[1, C]], 0, 0, allow_small_or_imprecise_dtypes=True)
+    op("g", "iota", [], ["ti"], T.ti[:], [[1, C]], 128, -1)
+    op("g", "iota", [], ["c16"], T.c16[:], [[16, 20]], 0, 0)
+    op("g", "iota", [], ["pa"], T.pa[:], [[0, 2]], 0, 1)
+    op("v", "set", [], ["ones"], T.ones[:], 1.0)
+    op("g", "sel", ["ones"], ["eb"], T.eb[:], T.ones[:], [[1, 520]], A.is_equal, 0.0, -3, -4)
+    for i in range(4):
+        op("v", "set", [], [("d%d" % i, -1)], T["d%d" % i][:, 0:PADZ], 0.0)
+    op("v", "set", [], ["iotc2"], T.iotc[:, C:C + 8], float(C))
+    op("v", "set", [], ["rw2"], T.rw[:, C:C + 8], float(C - 1))
+    op("v", "ts", ["iotj"], ["iotc"], T.iotc[:, 0:C], T.iotj[:], FRAC, None, A.add)
+    for n in ("hp", "iv", "mt"):
+        op("v", "copy", [n + "in"], [n + "o"], T[n + "o"][:], T[n + "in"][:])
+    op("s", "act", ["iotc", "iotc2", "hpo"], ["hpw"], T.hpw[:], T.iotc[:, 0:328].indirect(T.hpo[:]), F.Copy)
+    op("s", "act", ["iotj", "mto"], ["mtw"], T.mtw[:], T.iotj[:].indirect(T.mto[:]), F.Copy)
+    op("v", "ts", ["ti"], ["ti"], T.ti[:], T.ti[:], 15, None, A.bitwise_and)
+    op("v", "ts", ["pa"], ["pa"], T.pa[:], T.pa[:], 15, None, A.bitwise_and)
+    op("v", "ts", ["ti"], ["sce"], T.sce[:], T.ti[:], 0.0, LOW, A.is_equal, A.mult)
+    op("v", "ts", ["ti"], ["ew"], T.ew[:], T.ti[:], 1.0, BIG, A.is_equal, A.mult)
+    op("v", "copy", ["pa"], ["pf"], T.pf[:], T.pa[:])
+    op("v", "ts", ["pa"], ["bigc"], T.bigc[:], T.pa[:], 15.0, BIG, A.is_lt, A.mult)
+    op("v", "ts", ["pa"], ["bigs"], T.bigs[:], T.pa[:], 15.0, BIGS, A.is_lt, A.mult)
+    op("v", "tt", ["sce", "ew"], ["msk"], T.msk[:], T.sce[:], T.ew[:], A.add)
+    op("v", "ts", ["c16", "pf"], ["eif"], T.eif[:], T.c16[:], T.pf[:, 0:1], None, A.add)
+    op("v", "copy", ["ivin"], ["ivs"], T.ivs[:], T.ivin[:])
+    op("v", "ts", ["msk"], ["msks"], T.msks[:], T.msk[:], BIGS / BIG, LOWS, A.mult, A.max)
+    op("v", "ts", ["eif", "bigc"], ["cj"], T.cj[:], T.eif[:], T.bigc[:, 0:1], None, A.subtract)
+    for i in range(4):
+        nb = C // SIZES[i]
+        op("v", "ts", ["eif"], ["k%d" % i], T.kk[:, 20 * i:20 * i + 20], T.eif[:], -1.0 / nb, -(PADZ + 0.25) / nb, A.mult, A.add)
+    op("v", "ts", ["k0", "k1", "k2", "k3", "bigc"], ["k0", "k1", "k2", "k3"], T.kk[:], T.kk[:], T.bigc[:, 0:1], None, A.subtract)
+
+    def scan(dst, src, rd, lo=0):
+        op("v", "scan", rd + ["msk"], [dst], T[dst][:], T.msk[:], src, 0.0, A.add, A.max)
+
+    def ring():
+        op("v", "tt", ["hpw", "iotj"], ["rd0"], T.rd0[:], T.hpw[:], T.iotj[:], A.subtract); yield
+        op("v", "set", [], ["rd0"], T.rd0[:, C - 1:C], 0.0); yield
+        cur, nxt, off = "rd0", "rd1", "hpo"
+        for lev in range(9):
+            op("s", "act", [cur], ["rdc"], T.rdc[:], T[cur][:], F.Copy)
+            op("v", "tt", [cur, "rdc", off], [nxt], T[nxt][:], T[cur][:].indirect(T[off][:]), T.rdc[:], A.add); yield
+            if lev == 0:
+                op("v", "set", [], [nxt], T[nxt][:, C - 1:C], 0.0); yield
+            cur, nxt, off = nxt, cur, "rofs"
+            scan("rsc", T[cur][:], [cur]); yield
+            op("v", "tt", ["rsc", "cj"], ["rt"], T.rt[:], T.rsc[:, 15::16], T.cj[:], A.add); yield
+            if lev < 8:
+                op("v", "ts", ["rt"], ["rofs"], T.rofs[:], T.rt[:], 0.1, None, A.add); yield
+        op("v", "ts", ["rt"], ["pos"], T.pos[:], T.rt[:], -float(C - 1), 1024.0, A.add, A.mult); yield
+        op("v", "copy", ["pos"], ["poso"], T.poso[:], T.pos[:]); yield
+        op("v", "ts", ["pos"], ["peq"], T.peq[:], T.pos[:], 0.0, float(C), A.is_equal, A.mult); yield
+        op("v", "copy", ["iotj", "poso"], ["rw"], T.rw[:, 0:C].indirect(T.poso[:]), T.iotj[:]); yield
+        op("v", "tt", ["pos", "peq"], ["peq"], T.peq[:], T.pos[:], T.peq[:], A.add); yield
+        op("v", "ts", ["peq"], ["pmo"], T.pmo[:], T.peq[:], -1.0, None, A.add); yield
+        scan("rsc", T.rw[:, 0:C], ["rw"]); yield
+        op("v", "tt", ["rw", "rw2"], ["wd"], T.wd[:], T.rw[:, 0:C], T.rw[:, 1:C + 1], A.subtract); yield
+        op("v", "ts", ["rsc", "bigc"], ["rt"], T.rt[:], T.rsc[:, 15::16], T.bigc[:, 0:1], -1.0, A.subtract, A.mult); yield
+        op("v", "ts", ["rt"], ["ordo"], T.ordo[:], T.rt[:], float(PADZ + C - 1), None, A.add); yield
+
+    def alt(z, le, o):
+        op("v", "tt", [z, "eif"], ["xle"], T.xle[:], T[z][:], T.eif[:], A.is_le); yield
+        op("v", "ts", ["xle"], ["xle"], T.xle[:], T.xle[:], 1000.0, None, A.mult); yield
+        op("v", "tt", ["xle", z], ["xle"], T.xle[:], T.xle[:], T[z][:], A.add); yield
+        op("v", "ts", ["xle"], [o], T[o][:], T.xle[:], float(C), None, A.min); yield
+
+    def tables():
+        op("s", "act", ["mtw", "ivo"], ["ivmw"], T.ivmw[:], T.mtw[:].indirect(T.ivo[:]), F.Copy)
+        yield from alt("ivs", "xle", "xao")
+        scan("sc", T.ivmw[:], ["ivmw"]); yield
+        op("v", "ts", ["sc", "bigc"], ["t1"], T.t1[:], T.sc[:, 15::16], T.bigc[:, 0:1], None, A.subtract); yield
+        yield from alt("t1", "xle", "xbo")
+        op("v", "tt", ["t1", "ivs"], ["ivd"], T.ivd[:], T.t1[:], T.ivs[:], A.subtract); yield
+        op("s", "act", ["iotc", "iotc2", "xao"], ["xa"], T.xa[:], T.iotc[:, 0:328].indirect(T.xao[:]), F.Copy)
+        op("s", "act", ["iotc", "iotc2", "xbo"], ["xb"], T.xb[:], T.iotc[:, 0:328].indirect(T.xbo[:]), F.Copy)
+        op("v", "tt", ["xa", "iotj"], ["da"], T.da[:], T.xa[:], T.iotj[:], A.subtract); yield
+        op("v", "tt", ["xb", "xa"], ["dd"], T.dd[:], T.xb[:], T.xa[:], A.subtract); yield
+
+    def udtables():
+        op("v", "copy", ["udin"], ["udo"], T.udo[:], T.udin[:]); yield
+        op("v", "copy", ["udin"], ["uds"], T.uds[:], T.udin[:]); yield
+        op("s", "act", ["iotj", "udo"], ["xa"], T.xa[:], T.iotj[:].indirect(T.udo[:]), F.Copy)
+        op("s", "act", ["xa", "mto"], ["xb"], T.xb[:], T.xa[:].indirect(T.mto[:]), F.Copy)
+        scan("sce", T.xb[:], ["xb"]); yield
+        op("v", "ts", ["sce", "bigc"], ["sn"], T.sn[:], T.sce[:, 15::16], T.bigc[:, 0:1], None, A.subtract); yield
+        op("v", "tt", ["sn", "uds"], ["udd"], T.udd[:], T.sn[:], T.uds[:], A.subtract); yield
+
+    def run(main, *side):
+        side = [s for s in side]
+        for _ in main:
+            while side:
+                try:
+                    next(side[0])
+                    break
+                except StopIteration:
+                    side.pop(0)
+        for s in side:
+            for _ in s:
+                pass
+
+    def quantise_x(k, tile):
+        op("v", "quant", [tile], ["qx%d" % k, "sx%d" % k], T["qx%d" % k][:], T["sx%d" % k][:], T[tile][:])
+
+    def mm(bank, w, ws, x, xs, wv, wsv, xv, xsv, n):
+        op("t", "mm", [w, ws, x, xs], ["ps%d" % bank], T["ps%d" % bank][:, 0:n], wv, wsv, xv, xsv, True, True)
+
+    def unpack(bank, i, qn, sn):
+        mm(bank, "qe%d" % i, "se%d" % i, qn, sn, T.qe[:, 128 * i:128 * i + 128], T.se[:, 128 * i:128 * i + 128], T[qn][:], T[sn][:], C)
+
+    def th_copy(dst, i, bank):
+        op("s", "act", ["ps%d" % bank], [(dst, i)], T[dst][:, C * i:C * i + C], T["ps%d" % bank][:, 0:C], F.Copy, scale=0.5)
+
+    def pick(dst, src, i, off):
+        op("s", "act", [(src, i), off], [(dst, i)], T[dst][:, C * i:C * i + C], T[src][:, C * i:C * i + C].indirect(li(off)), F.Copy)
+
+    OWNB, PARB = [1, 2, 3, 4], [5, 6, 7, 0]
+
+    def keys(s, sets):
+        return [("d%d" % s, k) for k in sets]
+
+    def stage(s):
+        w = C // RAD[s]
+        nb = C // SIZES[s]
+        if w // 16 % 2:
+            op("v", "ts", ["t1"], ["ob"], T.ob[:, 1:21], T.t1[:], -float(nb), None, A.mult); yield
+        op("v", "ts", ["t1"], ["oa"], T.oa[:, 0:20], T.t1[:], -float(nb), None, A.mult); yield
+        for k in range(1, RAD[s]):
+            c0 = k * w // 16
+            o, lo = ("oa", c0) if c0 % 2 == 0 else ("ob", c0 + 1)
+            d = T["d%d" % s]
+            lim = PADZ + k * w
+            op("v", "tt", keys(s, range(-1, k + 1)) + [o], keys(s, [k]), d[:, lim:lim + w], d[:, 0:lim].indirect(T[o][:, lo:lo + w // 16]), d[:, lim:lim + w], A.add); yield
+
+    def turn(s):
+        q = RAD[s + 1]
+        w = C // q
+        for i in range(q):
+            op("v", "scan", keys(s, range(RAD[s])) + ["msk"], [("sc", i)] + (["sc"] if i == 0 else []), T.sc[:, w * i:w * i + w], T.msk[:, 0:w], T["d%d" % s][:, PADZ + q - 1 - i:PADZ + C:q], 0.0, A.add, A.max); yield
+            op("s", "act", keys(s, range(RAD[s])), keys(s + 1, [i]), T["d%d" % (s + 1)][:, PADZ + w * i:PADZ + w * i + w], T["d%d" % s][:, PADZ + q - 1 - i:PADZ + C:q], F.Copy)
+        k = "k%d" % (s + 1)
+        op("v", "tt", [("sc", i) for i in range(q)] + ["sc", k], ["t1"], T.t1[:], T.sc[:, 15::16], T.kk[:, 20 * s + 20:20 * s + 40], A.add); yield
+
+    def edit_iv(r):
+        op("v", "scan", ["giv", "msks"], ["scs"], T.scs[:], T.msks[:], T.giv[:], 0.0, A.add, A.max); yield
+        op("v", "ts", ["scs", "bigs"], ["sf"], T.sf[:], T.scs[:, 15::16], T.bigs[:, 0:1], None, A.subtract); yield
+        op("v", "tt", ["sf", "ivd"], ["sm"], T.sm[:], T.sf[:], T.ivd[:], A.mult); yield
+        op("v", "tt", ["ivs", "sm"], ["ivs"], T.ivs[:], T.ivs[:], T.sm[:], A.add); yield
+        op("v", "copy", ["ivs"], ["ivn%d" % r], li("ivn%d" % r), T.ivs[:])
+        send(rank ^ STEP[r], "ivn%d" % r, li("ivp%d" % r), li("ivn%d" % r), "ai%d" % r); yield
+        if r < 2:
+            op("v", "ts", ["sm"], ["sn"], T.sn[:], T.sm[:], -2.0, None, A.mult); yield
+            op("v", "tt", ["ivd", "sn"], ["ivd"], T.ivd[:], T.ivd[:], T.sn[:], A.add); yield
+
+    def edit_ud(r):
+        op("v", "scan", ["sw", "msks"], ["scs"], T.scs[:], T.msks[:], T.sw[:], 0.0, A.add, A.max); yield
+        op("v", "ts", ["scs", "bigs"], ["sf"], T.sf[:], T.scs[:, 15::16], T.bigs[:, 0:1], None, A.subtract); yield
+        op("v", "tt", ["sf", "udd"], ["sm"], T.sm[:], T.sf[:], T.udd[:], A.mult); yield
+        op("v", "tt", ["uds", "sm"], ["uds"], T.uds[:], T.uds[:], T.sm[:], A.add); yield
+        op("v", "copy", ["uds"], ["udn"], T.udn[:], T.uds[:]); yield
+        if r < 2:
+            op("v", "ts", ["sm"], ["sn"], T.sn[:], T.sm[:], -2.0, None, A.mult); yield
+            op("v", "tt", ["udd", "sn"], ["udd"], T.udd[:], T.udd[:], T.sn[:], A.add); yield
+
+    def signs(r):
+        ivo = "ivo" if r == 0 else "ivn%d" % (r - 1)
+        op("v", "ts", ["ps0"], ["pp"], T.pp[:], T.ps0[:, 0:C], 0.0, None, A.is_le); yield
+        op("s", "act", ["ps5"], ["sg"], T.sg[:], T.ps5[:, 0:C], F.Sign)
+        op("v", "tt", ["pp", "mto", "sg"], ["sw"], T.sw[:], T.pp[:].indirect(T.mto[:]), T.sg[:], A.is_lt); yield
+        op("s", "act", ["sw", ivo], ["giv"], T.giv[:], T.sw[:].indirect(li(ivo)), F.Copy)
+        op("v", "tt", ["sw", ivo, "dd"], ["tt"], T.tt[:], T.sw[:].indirect(li(ivo)), T.dd[:], A.mult); yield
+        for i in range(4):
+            op("v", "tt", ["tt", "da"], keys(0, [i]), T.d0[:, PADZ + 80 * i:PADZ + 80 * i + 80], T.tt[:, 3 - i::4], T.da[:, 3 - i::4], A.add); yield
+        op("v", "scan", keys(0, range(4)) + ["msk"], ["sc"] + [("sc", i) for i in range(5)], T.sc[:], T.msk[:], T.d0[:, PADZ:PADZ + C], 0.0, A.add, A.max); yield
+        op("v", "tt", ["sc", "k0"], ["t1"], T.t1[:], T.sc[:, 15::16], T.kk[:, 0:20], A.add); yield
+
+    def undos(r):
+        qp, sp = "qp%d" % r, "sp%d" % r
+        th_copy("th", 0, OWNB[0])
+        th_copy("th", 1, OWNB[1])
+        yield from stage(0)
+        yield from turn(0)
+        th_copy("th", 2, OWNB[2])
+        th_copy("th", 3, OWNB[3])
+        yield from stage(1)
+        yield from turn(1)
+        for i in range(4):
+            unpack(PARB[i], i, qp, sp)
+        yield from stage(2)
+        yield from turn(2)
+        for i in range(4):
+            th_copy("thp", i, PARB[i])
+        yield from stage(3)
+        for i in range(4):
+            pick("tiv", "thp", i, "ivp%d" % r)
+
+    def bypass(r):
+        op("v", "ts", keys(3, range(-1, 5)) + ["ordo"], ["vi"], T.vi[:], T.d3[:, 0:PADZ + C].indirect(T.ordo[:]), 1024.0, None, A.mult); yield
+        op("v", "ts", ["vi"], ["vi"], T.vi[:], T.vi[:], 1, None, A.bitwise_and); yield
+        op("v", "copy", ["vi"], ["ne"], T.ne[:], T.vi[:]); yield
+        op("v", "scan", ["ne", "wd"], ["st"], T.st[:], T.ne[:], T.wd[:], 0.0, A.mult, A.add); yield
+        op("v", "tt", ["st", "pmo", "iotj"], ["bw"], T.bw[:], T.st[:].indirect(T.pmo[:]), T.iotj[:], A.add); yield
+        scan("sce", T.bw[:], ["bw"]); yield
+        op("v", "ts", ["sce", "bigc"], ["bn%d" % r], li("bn%d" % r), T.sce[:, 15::16], T.bigc[:, 0:1], None, A.subtract)
+        send(rank ^ STEP[r], "bn%d" % r, li("bp%d" % r), li("bn%d" % r), "ab%d" % r); yield
+
+    def partner_e(r):
+        op("v", "copy", ["bw", "ivp%d" % r], ["ew"], T.ew[:], T.bw[:].indirect(li("ivp%d" % r))); yield
+        scan("sce", T.ew[:], ["ew"]); yield
+        op("v", "ts", ["sce", "bigc"], ["en%d" % r], li("en%d" % r), T.sce[:, 15::16], T.bigc[:, 0:1], None, A.subtract)
+        send(rank ^ STEP[r], "en%d" % r, li("ep%d" % r), li("en%d" % r), "ae%d" % r); yield
+
+    def keep_d(r):
+        op("v", "tt", ["da", "tt"], ["da"], T.da[:], T.da[:], T.tt[:], A.add); yield
+        op("v", "ts", ["tt"], ["ew"], T.ew[:], T.tt[:], -2.0, None, A.mult); yield
+        op("v", "tt", ["dd", "ew"], ["dd"], T.dd[:], T.dd[:], T.ew[:], A.add); yield
+
+    def flat(*gens):
+        for x in gens:
+            yield from x
+
+    op("v", "quant", ["uin"], ["qu", "su"], T.qu[:], T.su[:], T.uin[:])
+    op("v", "copy", ["c16"], ["uof"], T.uof[:], T.c16[:, 0:8])
+    op("v", "copy", ["qu", "uof"], ["qr"], T.qr[:].bitcast(dt.uint32), T.qu[:].bitcast(dt.uint32).indirect(T.uof[:]))
+    op("v", "copy", ["su", "uof"], ["sr"], T.sr[:], T.su[:].indirect(T.uof[:]))
+    for i in range(4):
+        op("v", "quant", ["eb"], ["qe%d" % i, "se%d" % i], T.qe[:, 128 * i:128 * i + 128], T.se[:, 128 * i:128 * i + 128], T.eb[:, 3 - i:3 - i + 512])
+    quantise_x(0, "xin")
+
+    for r in range(3):
+        p = rank ^ STEP[r]
+        qx, sx = "qx%d" % r, "sx%d" % r
+        send(p, qx, T["qp%d" % r][:].bitcast(dt.uint8), T[qx][:].bitcast(dt.uint8), "aq%d" % r)
+        send(p, sx, T["sp%d" % r][:], T[sx][:], "as%d" % r)
+        for bank in (0, 5):
+            mm(bank, "qr", "sr", qx, sx, T.qr[:], T.sr[:], T[qx][:], T[sx][:], C)
+        for i in range(4):
+            unpack(OWNB[i], i, qx, sx)
+        if r == 0:
+            rg = ring()
+            run(tables(), rg)
+            run(signs(0), rg)
+            run(undos(0), flat(edit_iv(0), rg, udtables(), edit_ud(0)))
+        else:
+            for _ in signs(r):
+                pass
+            run(undos(r), flat(edit_iv(r), edit_ud(r)))
+        for _ in bypass(r):
+            pass
+        for _ in partner_e(r):
+            pass
+        for i in range(4):
+            pick("tu", "th", i, "udn")
+        if r < 2:
+            for _ in keep_d(r):
+                pass
+        else:
+            op("s", "act", ["iotj", "udn"], ["xa"], T.xa[:], T.iotj[:].indirect(T.udn[:]), F.Copy)
+            dma("y", "duo", ["xa"], [], T.uo[:, :], T.xa[0:128:16, :])
+            op("v", "quant", ["vin"], ["qv_", "sv"], T.qv_[:], T.sv[:], T.vin[:])
+        for h in range(2):
+            for i in range(4):
+                c0 = 160 * h
+                op("v", "tt", [("thp", i), ("tiv", i), "bp%d" % r], [("zt", h, i)], T.zt[:, 4 * c0 + i:4 * c0 + 640:4],
+                   T.thp[:, C * i:C * i + C].indirect(li("bp%d" % r, 10 * h, 10 * h + 10)), T.tiv[:, C * i + c0:C * i + c0 + 160], A.add)
+            op("v", "quant", [("zt", h, i) for i in range(4)], ["qz%d" % h, "sz%d" % h], T.qz[:, 160 * h:160 * h + 160], T.sz[:, 160 * h:160 * h + 160], T.zt[:, 640 * h:640 * h + 640])
+            for i in range(4):
+                bank = (OWNB, PARB)[h][i]
+                mm(bank, "qw", "sw_", "qz%d" % h, "sz%d" % h, T.qw[:, 128 * i:128 * i + 128], T.sw_[:, 128 * i:128 * i + 128], T.qz[:, 160 * h:160 * h + 160], T.sz[:, 160 * h:160 * h + 160], 160)
+                op("s", "act", ["ps%d" % bank], [("hh", i, h)], T.hh[:, C * i + 160 * h:C * i + 160 * h + 160], T["ps%d" % bank][:, 0:160], F.Copy, scale=2.0 ** -6)
+        for i in range(4):
+            op("v", "tt", [("hh", i, 0), ("hh", i, 1), ("tu", i), "ep%d" % r], [("xt", i)], T.xt[:, i::4],
+               T.hh[:, C * i:C * i + C].indirect(li("ep%d" % r)), T.tu[:, C * i:C * i + C], A.add)
+        n = r + 1
+        op("v", "quant", [("xt", i) for i in range(4)], ["qx%d" % n, "sx%d" % n], T["qx%d" % n][:], T["sx%d" % n][:], T.xt[:])
+
+    dma("y", "doc", ["qx3"], [], T.oc[:], T.qx3[:].bitcast(dt.uint8))
+    for k in range(4):
+        dma("s" if k < 2 else "y", "ds%d" % k, ["sx3"], [], T.osc[4 * k:4 * k + 4, :], T.sx3[32 * k:32 * k + 4, :])
+    mm(0, "qv_", "sv", "qx3", "sx3", T.qv_[:], T.sv[:], T.qx3[:], T.sx3[:], C)
+    op("v", "copy", ["ps0"], ["ys"], T.ys[:], T.ps0[:, 0:C])
+    dma("y", "dy0", ["ys"], [], T.y[:], T.ys[:])
+    for s, n in total.items():
+        g.wait_ge(T.sem[s], n)

@@ -26,16 +26,16 @@ for _n in ("ud", "iv", "hp", "mt"):
 for _n in ("x", "u", "v", "wc", "ws", "y0", "y1", "oc", "s0", "s1", "s2", "s3", "uo"):
     SEMAPHORES.append("d" + _n)
 for _n, _w, _t in (("xin", 1280, BF), ("uin", 512, BF), ("vin", 512, BF), ("eb", 520, BF), ("ones", 520, BF),
-                   ("iotj", C, F32), ("iotc", 328, F32), ("ti", C, I32), ("c16", 20, I32), ("pa", 2, I32),
+                   ("iotj", C, F32), ("iotc", 328, F32), ("ti", 16, I32), ("c16", 20, I32), ("pa", 20, I32), ("po", 20, U16), ("m16", 32, F32),
                    ("msk", C, F32), ("msks", C, BF),
-                   ("pf", 2, F32), ("bigc", 2, F32), ("bigs", 2, F32), ("eif", 20, F32), ("cj", 20, F32), ("kk", 80, F32),
-                   ("hpw", C, F32), ("mtw", C, F32), ("ivmw", C, F32), ("xa", C, F32), ("xb", C, F32),
-                   ("rd0", C, F32), ("rd1", C, F32), ("rdc", C, F32), ("sg", C, F32), ("rsc", C, F32), ("rt", 20, F32), ("rofs", 20, U16), ("pos", 20, F32),
-                   ("poso", 20, U16), ("peq", 20, F32), ("pmo", 20, U16), ("rw", 328, F32), ("wd", C, F32), ("ordo", 20, U16),
+                   ("pf", 2, F32), ("bigc", 2, F32), ("bigs", 2, F32), ("eif", 20, F32), ("kk", 80, F32),
+                   ("mtw", C, F32), ("ivmw", C, F32), ("xa", C, F32), ("xb", C, F32),
+                   ("fa", 2 * C, F32), ("fb", 2 * C, F32), ("sg", C, F32), ("rsc", C, F32), ("rofs", 20, U16), ("wl", 16, F32), ("lo", 2, U16),
+                   ("lci", 4, I32), ("lc", 4, F32), ("ro", 20, U16), ("pw", C, F32), ("km", C, F32), ("pmo", 20, U16), ("rw", 328, F32), ("wd", C, F32), ("ordo", 20, U16),
                    ("da", C, F32), ("dd", C, F32), ("tt", C, F32), ("sc", C, F32), ("scs", C, BF), ("t1", 20, F32),
                    ("ivs", 20, F32), ("ivd", 20, F32), ("uds", 20, F32), ("udd", 20, F32), ("sf", 20, F32), ("sm", 20, F32), ("sn", 20, F32),
                    ("xle", 20, F32), ("xao", 20, U16), ("xbo", 20, U16), ("oa", 22, U16), ("ob", 22, U16),
-                   ("pp", C, BF), ("sw", C, BF), ("giv", C, BF), ("vi", C, I32), ("ne", C, F32), ("st", C, F32), ("bw", C, F32), ("ew", C, F32), ("sce", C, F32),
+                   ("pp", C, BF), ("sw", C, BF), ("giv", C, BF), ("vi", C, I32), ("st", C, F32), ("bw", C, F32), ("ew", C, F32), ("sce", C, F32),
                    ("th", 1280, BF), ("thp", 1280, BF), ("tiv", 1280, BF), ("tu", 1280, BF), ("hh", 1280, BF), ("xt", 1280, BF), ("zt", 1280, BF),
                    ("uof", 8, U16), ("ys", C, F32),
                    ("qu", 128, F4), ("su", 128, U8), ("qr", 128, F4), ("sr", 128, U8), ("qv_", 128, F4), ("sv", 128, U8),
@@ -86,7 +86,68 @@ def rank_program(g, core, T, topo):
             lastw[k] = [tok]
             readers[k] = []
 
+    rec, free, fin = [None], {q: 0.0 for q in eng}, {}
+    usual = {"copy": 0.1, "tt": 0.65, "ts": 0.1, "scan": 0.35, "set": 0.08, "quant": 0.2, "act": 0.6, "mm": 0.35, "iota": 0.8, "sel": 1.2}
+    small = ("t1", "sf", "sm", "sn", "ivs", "ivd", "uds", "udd", "xle")
+    quarter = [("sc", i) for i in range(5)] + [("d%d" % s, i) for s in range(4) for i in range(5)]
+
+    def start(q, rd, wr):
+        t = free[q]
+        for k in rd:
+            for x in lastw.get(k, ()):
+                t = max(t, fin.get(x, 0.0) + 0.06)
+        for k in wr:
+            for x in list(lastw.get(k, ())) + readers.get(k, []):
+                t = max(t, fin.get(x, 0.0) + 0.06)
+        return t
+
+    def lasts(name, wr):
+        if name == "tt" and wr[0] in small:
+            return 0.1
+        if wr and (wr[0] in quarter or wr[0] == "wl"):
+            return 0.2 if name == "tt" else 0.12
+        return usual[name]
+
+    def merge(*chains):
+        chains, done = [list(c) for c in chains], set()
+        while any(chains):
+            best = None
+            for c in chains:
+                while c and c[0][0] == "mark":
+                    done.add(c.pop(0)[1])
+                if c and c[0][0] == "after":
+                    if c[0][1] not in done:
+                        continue
+                    c.pop(0)
+                if c:
+                    f, a = c[0]
+                    t = start(a[0], a[2], a[3]) if f is op else (start(a[0], a[2], []) if f is dma else 0.0)
+                    if best is None or t < best[0] - 1e-6:
+                        best = (t, c)
+            if best is None:
+                continue
+            f, a = best[1].pop(0)
+            f(*a[:-1], **a[-1])
+
+    def chain(*parts):
+        out = []
+        for p in parts:
+            if isinstance(p, tuple):
+                out.append(p)
+                continue
+            rec[0] = out
+            for _ in p:
+                pass
+            rec[0] = None
+        return out
+
     def op(q, name, rd, wr, *a, **kw):
+        if rec[0] is not None:
+            rec[0].append((op, (q, name, rd, wr) + a + (kw,)))
+            return
+        t = start(q, rd, wr)
+        free[q] = t + lasts(name, wr)
+        fin[("q" + q, count["q" + q] + 1)] = free[q]
         need(q, rd, wr)
         f = {"copy": V.tensor_copy, "tt": V.tensor_tensor, "ts": V.tensor_scalar, "scan": V.tensor_tensor_scan, "set": V.memset,
              "quant": V.quantize_mx, "act": S.activation, "mm": P.matmul_mx, "iota": g.iota, "sel": g.affine_select}[name]
@@ -99,10 +160,15 @@ def rank_program(g, core, T, topo):
     def dma(q, sem, rd, wr, out, in_):
         need(q, rd, wr)
         total[sem] = total.get(sem, 0) + 16
+        free[q] += 0.06
+        fin[(sem, total[sem])] = free[q] + (3.5 if sem == "dx" else 2.2)
         eng[q].dma_start(out, in_).then_inc(T.sem[sem], 16)
         note((sem, total[sem]), rd, wr)
 
     def send(p, key, out, in_, sem):
+        if rec[0] is not None:
+            rec[0].append((send, (p, key, out, in_, sem, {})))
+            return
         need("g", [key], [])
         dst = T.cores[p]
         rid, pid = topo.addr(dst)[:2]
@@ -113,6 +179,7 @@ def rank_program(g, core, T, topo):
     def lands(key, sem, p):
         n = len(topo.engines(T.cores[p], core)[:8])
         lastw[key] = [(sem, n)]
+        fin[(sem, n)] = 14.0
         total[sem] = n
 
     for r in range(3):
@@ -137,64 +204,94 @@ def rank_program(g, core, T, topo):
     dma("y", "dv", [], ["vin"], T.vin[:], T.v[:])
 
     op("g", "iota", [], ["iotj"], T.iotj[:], [[1, C]], 0, 0, allow_small_or_imprecise_dtypes=True)
-    op("g", "iota", [], ["ti"], T.ti[:], [[1, C]], 128, -1)
+    op("g", "iota", [], ["ti"], T.ti[:], [[1, 16]], 128, -1)
+    op("g", "iota", [], ["pa"], T.pa[:], [[0, 20]], 0, 1)
     op("g", "iota", [], ["c16"], T.c16[:], [[16, 20]], 0, 0)
-    op("g", "iota", [], ["pa"], T.pa[:], [[0, 2]], 0, 1)
     op("v", "set", [], ["ones"], T.ones[:], 1.0)
     op("g", "sel", ["ones"], ["eb"], T.eb[:], T.ones[:], [[1, 520]], A.is_equal, 0.0, -3, -4)
-    for i in range(4):
-        op("v", "set", [], [("d%d" % i, -1)], T["d%d" % i][:, 0:PADZ], 0.0)
+    op("g", "iota", [], ["km"], T.km[:], [[1, C]], -1, 0, allow_small_or_imprecise_dtypes=True)
     op("v", "set", [], ["iotc2"], T.iotc[:, C:C + 8], float(C))
     op("v", "set", [], ["rw2"], T.rw[:, C:C + 8], float(C - 1))
-    op("v", "ts", ["iotj"], ["iotc"], T.iotc[:, 0:C], T.iotj[:], FRAC, None, A.add)
+    op("s", "act", ["iotj"], ["iotc"], T.iotc[:, 0:C], T.iotj[:], F.Copy, bias=FRAC)
     for n in ("hp", "iv", "mt"):
         op("v", "copy", [n + "in"], [n + "o"], T[n + "o"][:], T[n + "in"][:])
-    op("s", "act", ["iotc", "iotc2", "hpo"], ["hpw"], T.hpw[:], T.iotc[:, 0:328].indirect(T.hpo[:]), F.Copy)
+    op("s", "act", ["iotj", "hpo"], ["fa"], T.fa[:, 0:C], T.iotj[:].indirect(T.hpo[:]), F.Copy)
     op("s", "act", ["iotj", "mto"], ["mtw"], T.mtw[:], T.iotj[:].indirect(T.mto[:]), F.Copy)
     op("v", "ts", ["ti"], ["ti"], T.ti[:], T.ti[:], 15, None, A.bitwise_and)
     op("v", "ts", ["pa"], ["pa"], T.pa[:], T.pa[:], 15, None, A.bitwise_and)
-    op("v", "ts", ["ti"], ["sce"], T.sce[:], T.ti[:], 0.0, LOW, A.is_equal, A.mult)
-    op("v", "ts", ["ti"], ["ew"], T.ew[:], T.ti[:], 1.0, BIG, A.is_equal, A.mult)
-    op("v", "copy", ["pa"], ["pf"], T.pf[:], T.pa[:])
-    op("v", "ts", ["pa"], ["bigc"], T.bigc[:], T.pa[:], 15.0, BIG, A.is_lt, A.mult)
-    op("v", "ts", ["pa"], ["bigs"], T.bigs[:], T.pa[:], 15.0, BIGS, A.is_lt, A.mult)
-    op("v", "tt", ["sce", "ew"], ["msk"], T.msk[:], T.sce[:], T.ew[:], A.add)
-    op("v", "ts", ["c16", "pf"], ["eif"], T.eif[:], T.c16[:], T.pf[:, 0:1], None, A.add)
-    op("v", "copy", ["ivin"], ["ivs"], T.ivs[:], T.ivin[:])
-    op("v", "ts", ["msk"], ["msks"], T.msks[:], T.msk[:], BIGS / BIG, LOWS, A.mult, A.max)
-    op("v", "ts", ["eif", "bigc"], ["cj"], T.cj[:], T.eif[:], T.bigc[:, 0:1], None, A.subtract)
-    for i in range(4):
-        nb = C // SIZES[i]
-        op("v", "ts", ["eif"], ["k%d" % i], T.kk[:, 20 * i:20 * i + 20], T.eif[:], -1.0 / nb, -(PADZ + 0.25) / nb, A.mult, A.add)
-    op("v", "ts", ["k0", "k1", "k2", "k3", "bigc"], ["k0", "k1", "k2", "k3"], T.kk[:], T.kk[:], T.bigc[:, 0:1], None, A.subtract)
+    op("v", "copy", ["pa"], ["po"], T.po[:], T.pa[:])
+    op("v", "ts", ["ti"], ["sce"], T.sce[:, 0:16], T.ti[:], 0.0, LOW, A.is_equal, A.mult)
+    op("v", "ts", ["ti"], ["ew"], T.ew[:, 0:16], T.ti[:], 1.0, BIG, A.is_equal, A.mult)
+    op("v", "tt", ["sce", "ew"], ["m16"], T.m16[:, 0:16], T.sce[:, 0:16], T.ew[:, 0:16], A.add)
+    op("s", "act", ["m16", "po"], ["msk"], T.msk[:], T.m16[:, 0:16].indirect(T.po[:]), F.Copy)
+    op("v", "ts", ["m16"], ["m16s"], T.m16[:, 16:32], T.m16[:, 0:16], BIGS / BIG, LOWS, A.mult, A.max)
+    op("s", "act", ["m16s", "po"], ["msks"], T.msks[:], T.m16[:, 16:32].indirect(T.po[:]), F.Copy)
+    op("v", "copy", ["pa"], ["pf"], T.pf[:], T.pa[:, 0:2])
+    op("v", "ts", ["pa"], ["bigc"], T.bigc[:], T.pa[:, 0:2], 15.0, BIG, A.is_lt, A.mult)
+
+    def places():
+        op("v", "ts", ["c16", "pf"], ["eif"], T.eif[:], T.c16[:], T.pf[:, 0:1], None, A.add); yield
+        op("v", "copy", ["ivin"], ["ivs"], T.ivs[:], T.ivin[:]); yield
+
+    def places2():
+        for i in range(4):
+            op("v", "set", [], [("d%d" % i, -1)], T["d%d" % i][:, 0:PADZ], 0.0); yield
+        op("v", "ts", ["pa"], ["bigs"], T.bigs[:], T.pa[:, 0:2], 15.0, BIGS, A.is_lt, A.mult); yield
+        for i in range(4):
+            nb = C // SIZES[i]
+            op("v", "ts", ["eif"], ["k%d" % i], T.kk[:, 20 * i:20 * i + 20], T.eif[:], -1.0 / nb, -(PADZ + 0.25) / nb, A.mult, A.add); yield
+        op("v", "ts", ["k0", "k1", "k2", "k3", "bigc"], ["k0", "k1", "k2", "k3"], T.kk[:], T.kk[:], T.bigc[:, 0:1], None, A.subtract); yield
 
     def scan(dst, src, rd, lo=0):
         op("v", "scan", rd + ["msk"], [dst], T[dst][:], T.msk[:], src, 0.0, A.add, A.max)
 
     def ring():
-        op("v", "tt", ["hpw", "iotj"], ["rd0"], T.rd0[:], T.hpw[:], T.iotj[:], A.subtract); yield
-        op("v", "set", [], ["rd0"], T.rd0[:, C - 1:C], 0.0); yield
-        cur, nxt, off = "rd0", "rd1", "hpo"
-        for lev in range(9):
-            op("s", "act", [cur], ["rdc"], T.rdc[:], T[cur][:], F.Copy)
-            op("v", "tt", [cur, "rdc", off], [nxt], T[nxt][:], T[cur][:].indirect(T[off][:]), T.rdc[:], A.add); yield
-            if lev == 0:
-                op("v", "set", [], [nxt], T[nxt][:, C - 1:C], 0.0); yield
+        for n in ("fa", "fb"):
+            op("s", "act", ["iotj"], [n + "i"], T[n][:, C:2 * C], T.iotj[:], F.Copy)
+        op("v", "set", [], ["lo"], T.lo[:], float(C - 1)); yield
+        for k in range(4):
+            op("v", "ts", ["pa"], [("lci", k)], T.lci[:, k:k + 1], T.pa[:, 0:1], k, 1, A.logical_shift_right, A.bitwise_and); yield
+        op("v", "ts", [("lci", k) for k in range(4)] + ["bigc"], ["lc"], T.lc[:], T.lci[:], float(C), T.bigc[:, 0:1], A.mult, A.subtract); yield
+        cur, nxt, off = "fa", "fb", "hpo"
+
+        def part(src, keys_, n, outs):
+            op("v", "scan", keys_ + ["msk"], ["rsc"], T.rsc[:, 0:n], T.msk[:, 0:n], src, 0.0, A.add, A.max); yield
+            for k, o, c in outs:
+                op("v", "ts", ["rsc", "lc", "bigc"], [k], o, T.rsc[:, 15:n:16], c[0], None, c[1]); yield
+
+        minus = (T.bigc[:, 0:1], A.subtract)
+        op("s", "act", [cur, "lo"], ["wl"], T.wl[:], T[cur][:, 0:C].indirect(T.lo[:, 0:1]), F.Copy)
+        yield from part(T.wl[:], ["wl"], 16, [("lo", T.lo[:, 0:1], (T.lc[:, 0:1], A.add))])
+        for lev in range(8):
+            m = 1 << lev
+            if lev < 4:
+                dst, k = (T.wl[:], "wl") if lev < 3 else (T.rw[:, C - 16:C], ("rw", 16))
+                op("s", "act", [cur, cur + "i", "lo"], [k], dst, T[cur][:, 0:2 * C].indirect(T.lo[:, 0:1]), F.Copy)
+                outs = [("lo", T.lo[:, 0:1], (T.lc[:, lev + 1:lev + 2], A.add) if lev < 3 else minus)]
+                if lev == 3:
+                    outs.append(("ro", T.ro[:, 19:20], minus))
+                new = part(dst, [k], 16, outs)
+            if lev >= 4:
+                op("s", "act", [cur, off], [nxt], T[nxt][:, 0:C], T[cur][:, 0:C].indirect(T[off][:]), F.Copy)
+                if lev < 7:
+                    yield from part(T[nxt][:, 0:C], [nxt], C, [("rofs", T.rofs[:], minus)])
+                lst, lk = (T.lo[:, 0:1], "lo") if m == 16 else (T.ro[:, 20 - m // 16:20], "ro")
+                dst, k = T.rw[:, C - 2 * m:C - m], ("rw", 2 * m)
+                op("s", "act", [cur, lk], [k], dst, T[cur][:, 0:C].indirect(lst), F.Copy)
+                new = part(dst, [k], m, [("ro", T.ro[:, 20 - m // 8:20 - m // 16], minus)])
+            if lev < 4:
+                op("s", "act", [cur, off], [nxt], T[nxt][:, 0:C], T[cur][:, 0:C].indirect(T[off][:]), F.Copy)
+            yield from new
             cur, nxt, off = nxt, cur, "rofs"
-            scan("rsc", T[cur][:], [cur]); yield
-            op("v", "tt", ["rsc", "cj"], ["rt"], T.rt[:], T.rsc[:, 15::16], T.cj[:], A.add); yield
-            if lev < 8:
-                op("v", "ts", ["rt"], ["rofs"], T.rofs[:], T.rt[:], 0.1, None, A.add); yield
-        op("v", "ts", ["rt"], ["pos"], T.pos[:], T.rt[:], -float(C - 1), 1024.0, A.add, A.mult); yield
-        op("v", "copy", ["pos"], ["poso"], T.poso[:], T.pos[:]); yield
-        op("v", "ts", ["pos"], ["peq"], T.peq[:], T.pos[:], 0.0, float(C), A.is_equal, A.mult); yield
-        op("v", "copy", ["iotj", "poso"], ["rw"], T.rw[:, 0:C].indirect(T.poso[:]), T.iotj[:]); yield
-        op("v", "tt", ["pos", "peq"], ["peq"], T.peq[:], T.pos[:], T.peq[:], A.add); yield
-        op("v", "ts", ["peq"], ["pmo"], T.pmo[:], T.peq[:], -1.0, None, A.add); yield
-        scan("rsc", T.rw[:, 0:C], ["rw"]); yield
-        op("v", "tt", ["rw", "rw2"], ["wd"], T.wd[:], T.rw[:, 0:C], T.rw[:, 1:C + 1], A.subtract); yield
-        op("v", "ts", ["rsc", "bigc"], ["rt"], T.rt[:], T.rsc[:, 15::16], T.bigc[:, 0:1], -1.0, A.subtract, A.mult); yield
-        op("v", "ts", ["rt"], ["ordo"], T.ordo[:], T.rt[:], float(PADZ + C - 1), None, A.add); yield
+            if lev < 4:
+                yield from part(T[cur][:, 0:C], [cur], C, [("rofs", T.rofs[:], minus)])
+        op("s", "act", [cur, "ro"], [("rw", 320)], T.rw[:, 0:64], T[cur][:, 0:C].indirect(T.ro[:, 16:20]), F.Copy)
+        yield from part(T.rw[:, 0:64], [("rw", 320)], 64, [("ro", T.ro[:, 0:4], minus)])
+        op("v", "set", [], ["km"], T.km[:, 0:1], float(C - 1)); yield
+        op("v", "copy", ["km", "ro"], ["pw"], T.pw[:].indirect(T.ro[:]), T.km[:]); yield
+        op("v", "ts", ["ro"], ["ordo"], T.ordo[:], T.ro[:], -1.0, float(PADZ + C - 1), A.mult, A.add); yield
+        yield from part(T.pw[:], ["pw"], C, [("pmo", T.pmo[:], minus)])
+        op("v", "tt", [("rw", n) for n in (16, 32, 64, 128, 256, 320)] + ["rw2"], ["wd"], T.wd[:], T.rw[:, 0:C], T.rw[:, 1:C + 1], A.subtract); yield
 
     def alt(z, le, o):
         op("v", "tt", [z, "eif"], ["xle"], T.xle[:], T[z][:], T.eif[:], A.is_le); yield
@@ -272,9 +369,11 @@ def rank_program(g, core, T, topo):
     def turn(s):
         q = RAD[s + 1]
         w = C // q
+        src, o, ks = (T.da, 0, ["da"]) if s < 0 else (T["d%d" % s], PADZ, keys(s, range(RAD[s])))
         for i in range(q):
-            op("v", "scan", keys(s, range(RAD[s])) + ["msk"], [("sc", i)] + (["sc"] if i == 0 else []), T.sc[:, w * i:w * i + w], T.msk[:, 0:w], T["d%d" % s][:, PADZ + q - 1 - i:PADZ + C:q], 0.0, A.add, A.max); yield
-            op("s", "act", keys(s, range(RAD[s])), keys(s + 1, [i]), T["d%d" % (s + 1)][:, PADZ + w * i:PADZ + w * i + w], T["d%d" % s][:, PADZ + q - 1 - i:PADZ + C:q], F.Copy)
+            v = src[:, o + q - 1 - i:o + C:q]
+            op("v", "scan", ks + ["msk"], [("sc", i)] + (["sc"] if i == 0 else []), T.sc[:, w * i:w * i + w], T.msk[:, 0:w], v, 0.0, A.add, A.max); yield
+            op("s", "act", ks, keys(s + 1, [i]), T["d%d" % (s + 1)][:, PADZ + w * i:PADZ + w * i + w], v, F.Copy)
         k = "k%d" % (s + 1)
         op("v", "tt", [("sc", i) for i in range(q)] + ["sc", k], ["t1"], T.t1[:], T.sc[:, 15::16], T.kk[:, 20 * s + 20:20 * s + 40], A.add); yield
 
@@ -306,10 +405,8 @@ def rank_program(g, core, T, topo):
         op("v", "tt", ["pp", "mto", "sg"], ["sw"], T.sw[:], T.pp[:].indirect(T.mto[:]), T.sg[:], A.is_lt); yield
         op("s", "act", ["sw", ivo], ["giv"], T.giv[:], T.sw[:].indirect(li(ivo)), F.Copy)
         op("v", "tt", ["sw", ivo, "dd"], ["tt"], T.tt[:], T.sw[:].indirect(li(ivo)), T.dd[:], A.mult); yield
-        for i in range(4):
-            op("v", "tt", ["tt", "da"], keys(0, [i]), T.d0[:, PADZ + 80 * i:PADZ + 80 * i + 80], T.tt[:, 3 - i::4], T.da[:, 3 - i::4], A.add); yield
-        op("v", "scan", keys(0, range(4)) + ["msk"], ["sc"] + [("sc", i) for i in range(5)], T.sc[:], T.msk[:], T.d0[:, PADZ:PADZ + C], 0.0, A.add, A.max); yield
-        op("v", "tt", ["sc", "k0"], ["t1"], T.t1[:], T.sc[:, 15::16], T.kk[:, 0:20], A.add); yield
+        op("v", "tt", ["tt", "da"], ["da"], T.da[:], T.da[:], T.tt[:], A.add); yield
+        yield from turn(-1)
 
     def undos(r):
         qp, sp = "qp%d" % r, "sp%d" % r
@@ -334,54 +431,54 @@ def rank_program(g, core, T, topo):
     def bypass(r):
         op("v", "ts", keys(3, range(-1, 5)) + ["ordo"], ["vi"], T.vi[:], T.d3[:, 0:PADZ + C].indirect(T.ordo[:]), 1024.0, None, A.mult); yield
         op("v", "ts", ["vi"], ["vi"], T.vi[:], T.vi[:], 1, None, A.bitwise_and); yield
-        op("v", "copy", ["vi"], ["ne"], T.ne[:], T.vi[:]); yield
-        op("v", "scan", ["ne", "wd"], ["st"], T.st[:], T.ne[:], T.wd[:], 0.0, A.mult, A.add); yield
+        op("v", "scan", ["vi", "wd"], ["st"], T.st[:], T.vi[:], T.wd[:], 0.0, A.mult, A.add); yield
         op("v", "tt", ["st", "pmo", "iotj"], ["bw"], T.bw[:], T.st[:].indirect(T.pmo[:]), T.iotj[:], A.add); yield
         scan("sce", T.bw[:], ["bw"]); yield
         op("v", "ts", ["sce", "bigc"], ["bn%d" % r], li("bn%d" % r), T.sce[:, 15::16], T.bigc[:, 0:1], None, A.subtract)
         send(rank ^ STEP[r], "bn%d" % r, li("bp%d" % r), li("bn%d" % r), "ab%d" % r); yield
 
     def partner_e(r):
-        op("v", "copy", ["bw", "ivp%d" % r], ["ew"], T.ew[:], T.bw[:].indirect(li("ivp%d" % r))); yield
+        op("s", "act", ["bw", "ivp%d" % r], ["ew"], T.ew[:], T.bw[:].indirect(li("ivp%d" % r)), F.Copy)
+        yield from edit_ud(r)
         scan("sce", T.ew[:], ["ew"]); yield
         op("v", "ts", ["sce", "bigc"], ["en%d" % r], li("en%d" % r), T.sce[:, 15::16], T.bigc[:, 0:1], None, A.subtract)
         send(rank ^ STEP[r], "en%d" % r, li("ep%d" % r), li("en%d" % r), "ae%d" % r); yield
-
-    def keep_d(r):
-        op("v", "tt", ["da", "tt"], ["da"], T.da[:], T.da[:], T.tt[:], A.add); yield
-        op("v", "ts", ["tt"], ["ew"], T.ew[:], T.tt[:], -2.0, None, A.mult); yield
-        op("v", "tt", ["dd", "ew"], ["dd"], T.dd[:], T.dd[:], T.ew[:], A.add); yield
 
     def flat(*gens):
         for x in gens:
             yield from x
 
-    op("v", "quant", ["uin"], ["qu", "su"], T.qu[:], T.su[:], T.uin[:])
-    op("v", "copy", ["c16"], ["uof"], T.uof[:], T.c16[:, 0:8])
-    op("v", "copy", ["qu", "uof"], ["qr"], T.qr[:].bitcast(dt.uint32), T.qu[:].bitcast(dt.uint32).indirect(T.uof[:]))
-    op("v", "copy", ["su", "uof"], ["sr"], T.sr[:], T.su[:].indirect(T.uof[:]))
-    for i in range(4):
-        op("v", "quant", ["eb"], ["qe%d" % i, "se%d" % i], T.qe[:, 128 * i:128 * i + 128], T.se[:, 128 * i:128 * i + 128], T.eb[:, 3 - i:3 - i + 512])
-    quantise_x(0, "xin")
+    def prepare():
+        quantise_x(0, "xin"); yield
+        op("v", "quant", ["uin"], ["qu", "su"], T.qu[:], T.su[:], T.uin[:])
+        op("v", "copy", ["c16"], ["uof"], T.uof[:], T.c16[:, 0:8])
+        op("v", "copy", ["qu", "uof"], ["qr"], T.qr[:].bitcast(dt.uint32), T.qu[:].bitcast(dt.uint32).indirect(T.uof[:]))
+        op("s", "act", ["su", "uof"], ["sr"], T.sr[:], T.su[:].indirect(T.uof[:]), F.Copy)
 
-    for r in range(3):
+    def constants():
+        for i in range(4):
+            op("v", "quant", ["eb"], ["qe%d" % i, "se%d" % i], T.qe[:, 128 * i:128 * i + 128], T.se[:, 128 * i:128 * i + 128], T.eb[:, 3 - i:3 - i + 512]); yield
+
+    def exchange(r):
         p = rank ^ STEP[r]
         qx, sx = "qx%d" % r, "sx%d" % r
         send(p, qx, T["qp%d" % r][:].bitcast(dt.uint8), T[qx][:].bitcast(dt.uint8), "aq%d" % r)
-        send(p, sx, T["sp%d" % r][:], T[sx][:], "as%d" % r)
+        send(p, sx, T["sp%d" % r][:], T[sx][:], "as%d" % r); yield
         for bank in (0, 5):
             mm(bank, "qr", "sr", qx, sx, T.qr[:], T.sr[:], T[qx][:], T[sx][:], C)
+
+    def own(r):
         for i in range(4):
-            unpack(OWNB[i], i, qx, sx)
+            unpack(OWNB[i], i, "qx%d" % r, "sx%d" % r); yield
+
+    for r in range(3):
         if r == 0:
-            rg = ring()
-            run(tables(), rg)
-            run(signs(0), rg)
-            run(undos(0), flat(edit_iv(0), rg, udtables(), edit_ud(0)))
+            merge(chain(ring()),
+                  chain(prepare(), exchange(0), ("mark", "x"), constants(), own(0), ("mark", "own")),
+                  chain(places(), tables(), places2(), ("after", "x"), signs(0), ("mark", "giv"), ("after", "own"), undos(0)),
+                  chain(("after", "giv"), edit_iv(0), udtables()))
         else:
-            for _ in signs(r):
-                pass
-            run(undos(r), flat(edit_iv(r), edit_ud(r)))
+            merge(chain(exchange(r), own(r), signs(r), ("mark", "giv"), undos(r)), chain(("after", "giv"), edit_iv(r)))
         for _ in bypass(r):
             pass
         for _ in partner_e(r):
@@ -389,8 +486,7 @@ def rank_program(g, core, T, topo):
         for i in range(4):
             pick("tu", "th", i, "udn")
         if r < 2:
-            for _ in keep_d(r):
-                pass
+            op("s", "act", ["tt"], ["sg"], T.sg[:], T.tt[:], F.Copy, scale=-2.0)
         else:
             op("s", "act", ["iotj", "udn"], ["xa"], T.xa[:], T.iotj[:].indirect(T.udn[:]), F.Copy)
             dma("y", "duo", ["xa"], [], T.uo[:, :], T.xa[0:128:16, :])
@@ -405,6 +501,8 @@ def rank_program(g, core, T, topo):
                 bank = (OWNB, PARB)[h][i]
                 mm(bank, "qw", "sw_", "qz%d" % h, "sz%d" % h, T.qw[:, 128 * i:128 * i + 128], T.sw_[:, 128 * i:128 * i + 128], T.qz[:, 160 * h:160 * h + 160], T.sz[:, 160 * h:160 * h + 160], 160)
                 op("s", "act", ["ps%d" % bank], [("hh", i, h)], T.hh[:, C * i + 160 * h:C * i + 160 * h + 160], T["ps%d" % bank][:, 0:160], F.Copy, scale=2.0 ** -6)
+        if r < 2:
+            op("v", "tt", ["dd", "sg"], ["dd"], T.dd[:], T.dd[:], T.sg[:], A.add)
         for i in range(4):
             op("v", "tt", [("hh", i, 0), ("hh", i, 1), ("tu", i), "ep%d" % r], [("xt", i)], T.xt[:, i::4],
                T.hh[:, C * i:C * i + C].indirect(li("ep%d" % r)), T.tu[:, C * i:C * i + C], A.add)

from concourse.bass import DstId, RemoteDMATransfer
from concourse.mybir import dt, AluOpType as A, ActivationFunctionType as F

C = 320
RAD = [4, 4, 4, 5]
SIZES = [4, 16, 64, 320]
STEP = [1, 2, 4]
PADZ = 16
BIG, LOW = 1024.0, -8192.0
BIGS, LOWS = 4.0, -64.0
FRAC = 1.0 / 1024.0
F4, U8, BF, F32, I32, U16 = "float8_e4m3fn_x4", "uint8", "bfloat16", "float32", "int32", "uint16"

SCRATCH = {}
SEMAPHORES = ["qv", "qs", "qt", "qg", "sent"]


def _buf(name, n, dtype):
    SCRATCH[name] = ("sbuf", [128, n], dtype)


for _n in ("ud", "iv", "hp", "mt"):
    _buf(_n + "in", 20, I32)
    _buf(_n + "o", 20, U16)
    SEMAPHORES.append("d" + _n)
for _n in ("x", "u", "v", "wc", "ws", "y0", "y1", "oc", "s0", "s1", "s2", "s3", "uo"):
    SEMAPHORES.append("d" + _n)
for _n, _w, _t in (("xin", 1280, BF), ("uin", 512, BF), ("vin", 512, BF), ("eb", 520, BF), ("ones", 520, BF),
                   ("iotj", C, F32), ("iotc", 328, F32), ("ti", 16, I32), ("c16", 20, I32), ("pa", 20, I32), ("po", 20, U16), ("m16", 32, F32),
                   ("msk", C, F32), ("msks", C, BF),
                   ("pf", 2, F32), ("bigc", 2, F32), ("bigs", 2, F32), ("eif", 20, F32), ("kk", 80, F32),
                   ("mtw", C, F32), ("ivmw", C, F32), ("xa", C, F32), ("xb", C, F32),
                   ("fa", 2 * C, F32), ("fb", 2 * C, F32), ("sg", C, F32), ("rsc", C, F32), ("rofs", 20, U16), ("wl", 16, F32), ("lo", 2, U16),
                   ("lci", 4, I32), ("lc", 4, F32), ("ro", 20, U16), ("pw", C, F32), ("km", C, F32), ("pmo", 20, U16), ("rw", 328, F32), ("wd", C, F32), ("ordo", 20, U16),
                   ("da", C, F32), ("dd", C, F32), ("tt", C, F32), ("sc", C, F32), ("scs", C, BF), ("t1", 20, F32),
                   ("ivs", 20, F32), ("ivd", 20, F32), ("uds", 20, F32), ("udd", 20, F32), ("sf", 20, F32), ("sm", 20, F32), ("sn", 20, F32),
                   ("xle", 20, F32), ("xao", 20, U16), ("xbo", 20, U16), ("oa", 22, U16), ("ob", 22, U16),
                   ("pp", C, BF), ("sw", C, BF), ("giv", C, BF), ("vi", C, I32), ("st", C, F32), ("bw", C, F32), ("ew", C, F32), ("sce", C, F32),
                   ("th", 1280, BF), ("thp", 1280, BF), ("tiv", 1280, BF), ("tu", 1280, BF), ("hh", 1280, BF), ("xt", 1280, BF), ("zt", 1280, BF),
                   ("uof", 8, U16), ("ys", C, F32),
                   ("qu", 128, F4), ("su", 128, U8), ("qr", 128, F4), ("sr", 128, U8), ("qv_", 128, F4), ("sv", 128, U8),
                   ("qw", 512, F4), ("sw_", 512, U8), ("qe", 512, F4), ("se", 512, U8), ("qz", C, F4), ("sz", C, U8), ("udn", 20, U16)):
    _buf(_n, _w, _t)
for _n in ("ivn", "ivp", "bn", "bp", "en", "ep"):
    _buf(_n, 72, U16)
for _i in range(4):
    _buf("d%d" % _i, 16 + C, F32)
    _buf("qx%d" % _i, C, F4)
    _buf("sx%d" % _i, C, U8)
for _i in range(3):
    _buf("qp%d" % _i, C, F4)
    _buf("sp%d" % _i, C, U8)
    SEMAPHORES += ["%s%d" % (_n, _i) for _n in ("aq", "as", "ai", "ab", "ae")]
for _i in range(8):
    SCRATCH["ps%d" % _i] = ("psum", [128, 512], F32)


def rank_program(g, core, T, topo):
    rank = T.rank_of(core)
    if rank is None:
        return
    V, S, P, Y = g.vector, g.scalar, g.tensor, g.sync
    eng = {"v": V, "s": S, "t": P, "g": g, "y": Y}
    count = {"qv": 0, "qs": 0, "qt": 0, "qg": 0}
    seen = {q: {} for q in eng}
    lastw, readers = {}, {}
    total = {}

    def need(q, rd, wr):
        dep = {}
        for k in rd:
            for s, n in lastw.get(k, ()):
                dep[s] = max(dep.get(s, 0), n)
        for k in wr:
            for s, n in list(lastw.get(k, ())) + readers.get(k, []):
                dep[s] = max(dep.get(s, 0), n)
        for s, n in dep.items():
            if seen[q].get(s, 0) < n:
                eng[q].wait_ge(T.sem[s], n)
                seen[q][s] = n

    def note(tok, rd, wr):
        for k in rd:
            readers.setdefault(k, []).append(tok)
        for k in wr:
            lastw[k] = [tok]
            readers[k] = []

    rec, free, fin = [None], {q: 0.0 for q in eng}, {}
    usual = {"copy": 0.1, "tt": 0.65, "ts": 0.1, "scan": 0.35, "set": 0.08, "quant": 0.2, "act": 0.6, "mm": 0.35, "iota": 0.8, "sel": 1.2}
    small = ("t1", "sf", "sm", "sn", "ivs", "ivd", "uds", "udd", "xle")
    quarter = [("sc", i) for i in range(5)] + [("d%d" % s, i) for s in range(4) for i in range(5)]

    def start(q, rd, wr):
        t = free[q]
        for k in rd:
            for x in lastw.get(k, ()):
                t = max(t, fin.get(x, 0.0) + 0.06)
        for k in wr:
            for x in list(lastw.get(k, ())) + readers.get(k, []):
                t = max(t, fin.get(x, 0.0) + 0.06)
        return t

    def lasts(name, wr):
        if name == "tt" and wr[0] in small:
            return 0.1
        if wr and (wr[0] in quarter or wr[0] == "wl"):
            return 0.2 if name == "tt" else 0.12
        return usual[name]

    def merge(*chains):
        chains, done = [list(c) for c in chains], set()
        while any(chains):
            best = None
            for c in chains:
                while c and c[0][0] == "mark":
                    done.add(c.pop(0)[1])
                if c and c[0][0] == "after":
                    if c[0][1] not in done:
                        continue
                    c.pop(0)
                if c:
                    f, a = c[0]
                    t = start(a[0], a[2], a[3]) if f is op else (start(a[0], a[2], []) if f is dma else 0.0)
                    if best is None or t < best[0] - 1e-6:
                        best = (t, c)
            if best is None:
                continue
            f, a = best[1].pop(0)
            f(*a[:-1], **a[-1])

    def chain(*parts):
        out = []
        for p in parts:
            if isinstance(p, tuple):
                out.append(p)
                continue
            rec[0] = out
            for _ in p:
                pass
            rec[0] = None
        return out

    def op(q, name, rd, wr, *a, **kw):
        if rec[0] is not None:
            rec[0].append((op, (q, name, rd, wr) + a + (kw,)))
            return
        t = start(q, rd, wr)
        free[q] = t + lasts(name, wr)
        fin[("q" + q, count["q" + q] + 1)] = free[q]
        need(q, rd, wr)
        f = {"copy": V.tensor_copy, "tt": V.tensor_tensor, "ts": V.tensor_scalar, "scan": V.tensor_tensor_scan, "set": V.memset,
             "quant": V.quantize_mx, "act": S.activation, "mm": P.matmul_mx, "iota": g.iota, "sel": g.affine_select}[name]
        s = "q" + q
        count[s] += 1
        f(*a, **kw).then_inc(T.sem[s], 1)
        total[s] = count[s]
        note((s, count[s]), rd, wr)

    def dma(q, sem, rd, wr, out, in_):
        need(q, rd, wr)
        total[sem] = total.get(sem, 0) + 16
        free[q] += 0.06
        fin[(sem, total[sem])] = free[q] + (3.5 if sem == "dx" else 2.2)
        eng[q].dma_start(out, in_).then_inc(T.sem[sem], 16)
        note((sem, total[sem]), rd, wr)

    def send(p, key, out, in_, sem):
        if rec[0] is not None:
            rec[0].append((send, (p, key, out, in_, sem, {})))
            return
        need("g", [key], [])
        dst = T.cores[p]
        rid, pid = topo.addr(dst)[:2]
        e = topo.engines(core, dst)[:8]
        total["sent"] = total.get("sent", 0) + len(e)
        g.remote_dma(out, in_, T.sem[sem], T.sem.sent, pid, rid, sum(1 << i for i in e))

    def lands(key, sem, p):
        n = len(topo.engines(T.cores[p], core)[:8])
        lastw[key] = [(sem, n)]
        fin[(sem, n)] = 14.0
        total[sem] = n

    for r in range(3):
        p = rank ^ STEP[r]
        for k, s in (("qp", "aq"), ("sp", "as"), ("ivp", "ai"), ("bp", "ab"), ("ep", "ae")):
            lands("%s%d" % (k, r), "%s%d" % (s, r), p)

    def li(name, lo=0, hi=20):
        if name[:-1] in ("ivn", "ivp", "bn", "bp", "en", "ep"):
            o = 24 * int(name[-1])
            return T[name[:-1]][:, o + lo:o + hi]
        return T[name][:, lo:hi]

    dma("y", "dhp", [], ["hpin"], T.hpin[:], T.hp[:])
    dma("s", "div", [], ["ivin"], T.ivin[:], T.iv[:])
    dma("y", "dx", [], ["xin"], T.xin[:], T.x[:])
    dma("s", "dmt", [], ["mtin"], T.mtin[:], T.mt[:])
    dma("y", "du", [], ["uin"], T.uin[:], T.u[:])
    dma("s", "dud", [], ["udin"], T.udin[:], T.ud[:])
    dma("y", "dws", [], ["sw_"], T.sw_[:], T.ws[:])
    dma("y", "dwc", [], ["qw"], T.qw[:].bitcast(dt.uint8), T.wc[:])
    dma("y", "dv", [], ["vin"], T.vin[:], T.v[:])

    op("g", "iota", [], ["iotj"], T.iotj[:], [[1, C]], 0, 0, allow_small_or_imprecise_dtypes=True)
    op("g", "iota", [], ["ti"], T.ti[:], [[1, 16]], 128, -1)
    op("g", "iota", [], ["pa"], T.pa[:], [[0, 20]], 0, 1)
    op("g", "iota", [], ["c16"], T.c16[:], [[16, 20]], 0, 0)
    op("v", "set", [], ["ones"], T.ones[:], 1.0)
    op("g", "sel", ["ones"], ["eb"], T.eb[:], T.ones[:], [[1, 520]], A.is_equal, 0.0, -3, -4)
    op("g", "iota", [], ["km"], T.km[:], [[1, C]], -1, 0, allow_small_or_imprecise_dtypes=True)
    op("v", "set", [], ["iotc2"], T.iotc[:, C:C + 8], float(C))
    op("v", "set", [], ["rw2"], T.rw[:, C:C + 8], float(C - 1))
    op("s", "act", ["iotj"], ["iotc"], T.iotc[:, 0:C], T.iotj[:], F.Copy, bias=FRAC)
    for n in ("hp", "iv", "mt"):
        op("v", "copy", [n + "in"], [n + "o"], T[n + "o"][:], T[n + "in"][:])
    op("s", "act", ["iotj", "hpo"], ["fa"], T.fa[:, 0:C], T.iotj[:].indirect(T.hpo[:]), F.Copy)
    op("s", "act", ["iotj", "mto"], ["mtw"], T.mtw[:], T.iotj[:].indirect(T.mto[:]), F.Copy)
    op("v", "ts", ["ti"], ["ti"], T.ti[:], T.ti[:], 15, None, A.bitwise_and)
    op("v", "ts", ["pa"], ["pa"], T.pa[:], T.pa[:], 15, None, A.bitwise_and)
    op("v", "copy", ["pa"], ["po"], T.po[:], T.pa[:])
    op("v", "ts", ["ti"], ["sce"], T.sce[:, 0:16], T.ti[:], 0.0, LOW, A.is_equal, A.mult)
    op("v", "ts", ["ti"], ["ew"], T.ew[:, 0:16], T.ti[:], 1.0, BIG, A.is_equal, A.mult)
    op("v", "tt", ["sce", "ew"], ["m16"], T.m16[:, 0:16], T.sce[:, 0:16], T.ew[:, 0:16], A.add)
    op("s", "act", ["m16", "po"], ["msk"], T.msk[:], T.m16[:, 0:16].indirect(T.po[:]), F.Copy)
    op("v", "ts", ["m16"], ["m16s"], T.m16[:, 16:32], T.m16[:, 0:16], BIGS / BIG, LOWS, A.mult, A.max)
    op("s", "act", ["m16s", "po"], ["msks"], T.msks[:], T.m16[:, 16:32].indirect(T.po[:]), F.Copy)
    op("v", "copy", ["pa"], ["pf"], T.pf[:], T.pa[:, 0:2])
    op("v", "ts", ["pa"], ["bigc"], T.bigc[:], T.pa[:, 0:2], 15.0, BIG, A.is_lt, A.mult)

    def places():
        op("v", "ts", ["c16", "pf"], ["eif"], T.eif[:], T.c16[:], T.pf[:, 0:1], None, A.add); yield
        op("v", "copy", ["ivin"], ["ivs"], T.ivs[:], T.ivin[:]); yield

    def places2():
        for i in range(4):
            op("v", "set", [], [("d%d" % i, -1)], T["d%d" % i][:, 0:PADZ], 0.0); yield
        op("v", "ts", ["pa"], ["bigs"], T.bigs[:], T.pa[:, 0:2], 15.0, BIGS, A.is_lt, A.mult); yield
        for i in range(4):
            nb = C // SIZES[i]
            op("v", "ts", ["eif"], ["k%d" % i], T.kk[:, 20 * i:20 * i + 20], T.eif[:], -1.0 / nb, -(PADZ + 0.25) / nb, A.mult, A.add); yield
        op("v", "ts", ["k0", "k1", "k2", "k3", "bigc"], ["k0", "k1", "k2", "k3"], T.kk[:], T.kk[:], T.bigc[:, 0:1], None, A.subtract); yield

    def scan(dst, src, rd, lo=0):
        op("v", "scan", rd + ["msk"], [dst], T[dst][:], T.msk[:], src, 0.0, A.add, A.max)

    def ring():
        for n in ("fa", "fb"):
            op("s", "act", ["iotj"], [n + "i"], T[n][:, C:2 * C], T.iotj[:], F.Copy)
        op("v", "set", [], ["lo"], T.lo[:], float(C - 1)); yield
        for k in range(4):
            op("v", "ts", ["pa"], [("lci", k)], T.lci[:, k:k + 1], T.pa[:, 0:1], k, 1, A.logical_shift_right, A.bitwise_and); yield
        op("v", "ts", [("lci", k) for k in range(4)] + ["bigc"], ["lc"], T.lc[:], T.lci[:], float(C), T.bigc[:, 0:1], A.mult, A.subtract); yield
        cur, nxt, off = "fa", "fb", "hpo"

        def part(src, keys_, n, outs):
            op("v", "scan", keys_ + ["msk"], ["rsc"], T.rsc[:, 0:n], T.msk[:, 0:n], src, 0.0, A.add, A.max); yield
            for k, o, c in outs:
                op("v", "ts", ["rsc", "lc", "bigc"], [k], o, T.rsc[:, 15:n:16], c[0], None, c[1]); yield

        minus = (T.bigc[:, 0:1], A.subtract)
        op("s", "act", [cur, "lo"], ["wl"], T.wl[:], T[cur][:, 0:C].indirect(T.lo[:, 0:1]), F.Copy)
        yield from part(T.wl[:], ["wl"], 16, [("lo", T.lo[:, 0:1], (T.lc[:, 0:1], A.add))])
        for lev in range(8):
            m = 1 << lev
            if lev < 4:
                dst, k = (T.wl[:], "wl") if lev < 3 else (T.rw[:, C - 16:C], ("rw", 16))
                op("s", "act", [cur, cur + "i", "lo"], [k], dst, T[cur][:, 0:2 * C].indirect(T.lo[:, 0:1]), F.Copy)
                outs = [("lo", T.lo[:, 0:1], (T.lc[:, lev + 1:lev + 2], A.add) if lev < 3 else minus)]
                if lev == 3:
                    outs.append(("ro", T.ro[:, 19:20], minus))
                new = part(dst, [k], 16, outs)
            if lev >= 4:
                op("s", "act", [cur, off], [nxt], T[nxt][:, 0:C], T[cur][:, 0:C].indirect(T[off][:]), F.Copy)
                if lev < 7:
                    yield from part(T[nxt][:, 0:C], [nxt], C, [("rofs", T.rofs[:], minus)])
                lst, lk = (T.lo[:, 0:1], "lo") if m == 16 else (T.ro[:, 20 - m // 16:20], "ro")
                dst, k = T.rw[:, C - 2 * m:C - m], ("rw", 2 * m)
                op("s", "act", [cur, lk], [k], dst, T[cur][:, 0:C].indirect(lst), F.Copy)
                new = part(dst, [k], m, [("ro", T.ro[:, 20 - m // 8:20 - m // 16], minus)])
            if lev < 4:
                op("s", "act", [cur, off], [nxt], T[nxt][:, 0:C], T[cur][:, 0:C].indirect(T[off][:]), F.Copy)
            yield from new
            cur, nxt, off = nxt, cur, "rofs"
            if lev < 4:
                yield from part(T[cur][:, 0:C], [cur], C, [("rofs", T.rofs[:], minus)])
        op("s", "act", [cur, "ro"], [("rw", 320)], T.rw[:, 0:64], T[cur][:, 0:C].indirect(T.ro[:, 16:20]), F.Copy)
        yield from part(T.rw[:, 0:64], [("rw", 320)], 64, [("ro", T.ro[:, 0:4], minus)])
        op("v", "set", [], ["km"], T.km[:, 0:1], float(C - 1)); yield
        op("v", "copy", ["km", "ro"], ["pw"], T.pw[:].indirect(T.ro[:]), T.km[:]); yield
        op("v", "ts", ["ro"], ["ordo"], T.ordo[:], T.ro[:], -1.0, float(PADZ + C - 1), A.mult, A.add); yield
        yield from part(T.pw[:], ["pw"], C, [("pmo", T.pmo[:], minus)])
        op("v", "tt", [("rw", n) for n in (16, 32, 64, 128, 256, 320)] + ["rw2"], ["wd"], T.wd[:], T.rw[:, 0:C], T.rw[:, 1:C + 1], A.subtract); yield

    def alt(z, le, o):
        op("v", "tt", [z, "eif"], ["xle"], T.xle[:], T[z][:], T.eif[:], A.is_le); yield
        op("v", "ts", ["xle"], ["xle"], T.xle[:], T.xle[:], 1000.0, None, A.mult); yield
        op("v", "tt", ["xle", z], ["xle"], T.xle[:], T.xle[:], T[z][:], A.add); yield
        op("v", "ts", ["xle"], [o], T[o][:], T.xle[:], float(C), None, A.min); yield

    def tables():
        op("s", "act", ["mtw", "ivo"], ["ivmw"], T.ivmw[:], T.mtw[:].indirect(T.ivo[:]), F.Copy)
        yield from alt("ivs", "xle", "xao")
        scan("sc", T.ivmw[:], ["ivmw"]); yield
        op("v", "ts", ["sc", "bigc"], ["t1"], T.t1[:], T.sc[:, 15::16], T.bigc[:, 0:1], None, A.subtract); yield
        yield from alt("t1", "xle", "xbo")
        op("v", "tt", ["t1", "ivs"], ["ivd"], T.ivd[:], T.t1[:], T.ivs[:], A.subtract); yield
        op("s", "act", ["iotc", "iotc2", "xao"], ["xa"], T.xa[:], T.iotc[:, 0:328].indirect(T.xao[:]), F.Copy)
        op("s", "act", ["iotc", "iotc2", "xbo"], ["xb"], T.xb[:], T.iotc[:, 0:328].indirect(T.xbo[:]), F.Copy)
        op("v", "tt", ["xa", "iotj"], ["da"], T.da[:], T.xa[:], T.iotj[:], A.subtract); yield
        op("v", "tt", ["xb", "xa"], ["dd"], T.dd[:], T.xb[:], T.xa[:], A.subtract); yield

    def udtables():
        op("v", "copy", ["udin"], ["udo"], T.udo[:], T.udin[:]); yield
        op("v", "copy", ["udin"], ["uds"], T.uds[:], T.udin[:]); yield
        op("s", "act", ["iotj", "udo"], ["xa"], T.xa[:], T.iotj[:].indirect(T.udo[:]), F.Copy)
        op("s", "act", ["xa", "mto"], ["xb"], T.xb[:], T.xa[:].indirect(T.mto[:]), F.Copy)
        scan("sce", T.xb[:], ["xb"]); yield
        op("v", "ts", ["sce", "bigc"], ["sn"], T.sn[:], T.sce[:, 15::16], T.bigc[:, 0:1], None, A.subtract); yield
        op("v", "tt", ["sn", "uds"], ["udd"], T.udd[:], T.sn[:], T.uds[:], A.subtract); yield

    def run(main, *side):
        side = [s for s in side]
        for _ in main:
            while side:
                try:
                    next(side[0])
                    break
                except StopIteration:
                    side.pop(0)
        for s in side:
            for _ in s:
                pass

    def quantise_x(k, tile):
        op("v", "quant", [tile], ["qx%d" % k, "sx%d" % k], T["qx%d" % k][:], T["sx%d" % k][:], T[tile][:])

    def mm(bank, w, ws, x, xs, wv, wsv, xv, xsv, n):
        op("t", "mm", [w, ws, x, xs], ["ps%d" % bank], T["ps%d" % bank][:, 0:n], wv, wsv, xv, xsv, True, True)

    def unpack(bank, i, qn, sn):
        mm(bank, "qe%d" % i, "se%d" % i, qn, sn, T.qe[:, 128 * i:128 * i + 128], T.se[:, 128 * i:128 * i + 128], T[qn][:], T[sn][:], C)

    def th_copy(dst, i, bank):
        op("s", "act", ["ps%d" % bank], [(dst, i)], T[dst][:, C * i:C * i + C], T["ps%d" % bank][:, 0:C], F.Copy, scale=0.5)

    def pick(dst, src, i, off):
        op("s", "act", [(src, i), off], [(dst, i)], T[dst][:, C * i:C * i + C], T[src][:, C * i:C * i + C].indirect(li(off)), F.Copy)

    OWNB, PARB = [1, 2, 3, 4], [5, 6, 7, 0]

    def keys(s, sets):
        return [("d%d" % s, k) for k in sets]

    def stage(s):
        w = C // RAD[s]
        nb = C // SIZES[s]
        if w // 16 % 2:
            op("v", "ts", ["t1"], ["ob"], T.ob[:, 1:21], T.t1[:], -float(nb), None, A.mult); yield
        op("v", "ts", ["t1"], ["oa"], T.oa[:, 0:20], T.t1[:], -float(nb), None, A.mult); yield
        for k in range(1, RAD[s]):
            c0 = k * w // 16
            o, lo = ("oa", c0) if c0 % 2 == 0 else ("ob", c0 + 1)
            d = T["d%d" % s]
            lim = PADZ + k * w
            op("v", "tt", keys(s, range(-1, k + 1)) + [o], keys(s, [k]), d[:, lim:lim + w], d[:, 0:lim].indirect(T[o][:, lo:lo + w // 16]), d[:, lim:lim + w], A.add); yield

    def turn(s):
        q = RAD[s + 1]
        w = C // q
        src, o, ks = (T.da, 0, ["da"]) if s < 0 else (T["d%d" % s], PADZ, keys(s, range(RAD[s])))
        for i in range(q):
            v = src[:, o + q - 1 - i:o + C:q]
            op("v", "scan", ks + ["msk"], [("sc", i)] + (["sc"] if i == 0 else []), T.sc[:, w * i:w * i + w], T.msk[:, 0:w], v, 0.0, A.add, A.max); yield
            op("s", "act", ks, keys(s + 1, [i]), T["d%d" % (s + 1)][:, PADZ + w * i:PADZ + w * i + w], v, F.Copy)
        k = "k%d" % (s + 1)
        op("v", "tt", [("sc", i) for i in range(q)] + ["sc", k], ["t1"], T.t1[:], T.sc[:, 15::16], T.kk[:, 20 * s + 20:20 * s + 40], A.add); yield

    def edit_iv(r):
        op("v", "scan", ["giv", "msks"], ["scs"], T.scs[:], T.msks[:], T.giv[:], 0.0, A.add, A.max); yield
        op("v", "ts", ["scs", "bigs"], ["sf"], T.sf[:], T.scs[:, 15::16], T.bigs[:, 0:1], None, A.subtract); yield
        op("v", "tt", ["sf", "ivd"], ["sm"], T.sm[:], T.sf[:], T.ivd[:], A.mult); yield
        op("v", "tt", ["ivs", "sm"], ["ivs"], T.ivs[:], T.ivs[:], T.sm[:], A.add); yield
        op("v", "copy", ["ivs"], ["ivn%d" % r], li("ivn%d" % r), T.ivs[:])
        send(rank ^ STEP[r], "ivn%d" % r, li("ivp%d" % r), li("ivn%d" % r), "ai%d" % r); yield
        if r < 2:
            op("v", "ts", ["sm"], ["sn"], T.sn[:], T.sm[:], -2.0, None, A.mult); yield
            op("v", "tt", ["ivd", "sn"], ["ivd"], T.ivd[:], T.ivd[:], T.sn[:], A.add); yield

    def edit_ud(r):
        op("v", "scan", ["sw", "msks"], ["scs"], T.scs[:], T.msks[:], T.sw[:], 0.0, A.add, A.max); yield
        op("v", "ts", ["scs", "bigs"], ["sf"], T.sf[:], T.scs[:, 15::16], T.bigs[:, 0:1], None, A.subtract); yield
        op("v", "tt", ["sf", "udd"], ["sm"], T.sm[:], T.sf[:], T.udd[:], A.mult); yield
        op("v", "tt", ["uds", "sm"], ["uds"], T.uds[:], T.uds[:], T.sm[:], A.add); yield
        op("v", "copy", ["uds"], ["udn"], T.udn[:], T.uds[:]); yield
        if r < 2:
            op("v", "ts", ["sm"], ["sn"], T.sn[:], T.sm[:], -2.0, None, A.mult); yield
            op("v", "tt", ["udd", "sn"], ["udd"], T.udd[:], T.udd[:], T.sn[:], A.add); yield

    def signs(r):
        ivo = "ivo" if r == 0 else "ivn%d" % (r - 1)
        op("v", "ts", ["ps0"], ["pp"], T.pp[:], T.ps0[:, 0:C], 0.0, None, A.is_le); yield
        op("s", "act", ["ps5"], ["sg"], T.sg[:], T.ps5[:, 0:C], F.Sign)
        op("v", "tt", ["pp", "mto", "sg"], ["sw"], T.sw[:], T.pp[:].indirect(T.mto[:]), T.sg[:], A.is_lt); yield
        op("s", "act", ["sw", ivo], ["giv"], T.giv[:], T.sw[:].indirect(li(ivo)), F.Copy)
        op("v", "tt", ["sw", ivo, "dd"], ["tt"], T.tt[:], T.sw[:].indirect(li(ivo)), T.dd[:], A.mult); yield
        op("v", "tt", ["tt", "da"], ["da"], T.da[:], T.da[:], T.tt[:], A.add); yield
        yield from turn(-1)

    def undos(r):
        qp, sp = "qp%d" % r, "sp%d" % r
        th_copy("th", 0, OWNB[0])
        th_copy("th", 1, OWNB[1])
        yield from stage(0)
        yield from turn(0)
        th_copy("th", 2, OWNB[2])
        th_copy("th", 3, OWNB[3])
        yield from stage(1)
        yield from turn(1)
        for i in range(4):
            unpack(PARB[i], i, qp, sp)
        yield from stage(2)
        yield from turn(2)
        for i in range(4):
            th_copy("thp", i, PARB[i])
        yield from stage(3)
        for i in range(4):
            pick("tiv", "thp", i, "ivp%d" % r)

    def bypass(r):
        op("v", "ts", keys(3, range(-1, 5)) + ["ordo"], ["vi"], T.vi[:], T.d3[:, 0:PADZ + C].indirect(T.ordo[:]), 1024.0, None, A.mult); yield
        op("v", "ts", ["vi"], ["vi"], T.vi[:], T.vi[:], 1, None, A.bitwise_and); yield
        op("v", "scan", ["vi", "wd"], ["st"], T.st[:], T.vi[:], T.wd[:], 0.0, A.mult, A.add); yield
        op("v", "tt", ["st", "pmo", "iotj"], ["bw"], T.bw[:], T.st[:].indirect(T.pmo[:]), T.iotj[:], A.add); yield
        scan("sce", T.bw[:], ["bw"]); yield
        op("v", "ts", ["sce", "bigc"], ["bn%d" % r], li("bn%d" % r), T.sce[:, 15::16], T.bigc[:, 0:1], None, A.subtract)
        send(rank ^ STEP[r], "bn%d" % r, li("bp%d" % r), li("bn%d" % r), "ab%d" % r); yield

    def partner_e(r):
        op("s", "act", ["bw", "ivp%d" % r], ["ew"], T.ew[:], T.bw[:].indirect(li("ivp%d" % r)), F.Copy)
        yield from edit_ud(r)
        scan("sce", T.ew[:], ["ew"]); yield
        op("v", "ts", ["sce", "bigc"], ["en%d" % r], li("en%d" % r), T.sce[:, 15::16], T.bigc[:, 0:1], None, A.subtract)
        send(rank ^ STEP[r], "en%d" % r, li("ep%d" % r), li("en%d" % r), "ae%d" % r); yield

    def flat(*gens):
        for x in gens:
            yield from x

    def prepare():
        quantise_x(0, "xin"); yield
        op("v", "quant", ["uin"], ["qu", "su"], T.qu[:], T.su[:], T.uin[:])
        op("v", "copy", ["c16"], ["uof"], T.uof[:], T.c16[:, 0:8])
        op("v", "copy", ["qu", "uof"], ["qr"], T.qr[:].bitcast(dt.uint32), T.qu[:].bitcast(dt.uint32).indirect(T.uof[:]))
        op("s", "act", ["su", "uof"], ["sr"], T.sr[:], T.su[:].indirect(T.uof[:]), F.Copy)

    def constants():
        for i in range(4):
            op("v", "quant", ["eb"], ["qe%d" % i, "se%d" % i], T.qe[:, 128 * i:128 * i + 128], T.se[:, 128 * i:128 * i + 128], T.eb[:, 3 - i:3 - i + 512]); yield

    def exchange(r):
        p = rank ^ STEP[r]
        qx, sx = "qx%d" % r, "sx%d" % r
        send(p, qx, T["qp%d" % r][:].bitcast(dt.uint8), T[qx][:].bitcast(dt.uint8), "aq%d" % r)
        send(p, sx, T["sp%d" % r][:], T[sx][:], "as%d" % r); yield
        for bank in (0, 5):
            mm(bank, "qr", "sr", qx, sx, T.qr[:], T.sr[:], T[qx][:], T[sx][:], C)

    def own(r):
        for i in range(4):
            unpack(OWNB[i], i, "qx%d" % r, "sx%d" % r); yield

    for r in range(3):
        if r == 0:
            merge(chain(ring()),
                  chain(prepare(), exchange(0), ("mark", "x"), constants(), own(0), ("mark", "own")),
                  chain(places(), tables(), places2(), ("after", "x"), signs(0), ("mark", "giv"), ("after", "own"), undos(0)),
                  chain(("after", "giv"), edit_iv(0), udtables()))
        else:
            merge(chain(exchange(r), own(r), signs(r), ("mark", "giv"), undos(r)), chain(("after", "giv"), edit_iv(r)))
        for _ in bypass(r):
            pass
        for _ in partner_e(r):
            pass
        for i in range(4):
            pick("tu", "th", i, "udn")
        if r < 2:
            op("s", "act", ["tt"], ["sg"], T.sg[:], T.tt[:], F.Copy, scale=-2.0)
        else:
            op("s", "act", ["iotj", "udn"], ["xa"], T.xa[:], T.iotj[:].indirect(T.udn[:]), F.Copy)
            dma("y", "duo", ["xa"], [], T.uo[:, :], T.xa[0:128:16, :])
            op("v", "quant", ["vin"], ["qv_", "sv"], T.qv_[:], T.sv[:], T.vin[:])
        for h in range(2):
            for i in range(4):
                c0 = 160 * h
                op("v", "tt", [("thp", i), ("tiv", i), "bp%d" % r], [("zt", h, i)], T.zt[:, 4 * c0 + i:4 * c0 + 640:4],
                   T.thp[:, C * i:C * i + C].indirect(li("bp%d" % r, 10 * h, 10 * h + 10)), T.tiv[:, C * i + c0:C * i + c0 + 160], A.add)
            op("v", "quant", [("zt", h, i) for i in range(4)], ["qz%d" % h, "sz%d" % h], T.qz[:, 160 * h:160 * h + 160], T.sz[:, 160 * h:160 * h + 160], T.zt[:, 640 * h:640 * h + 640])
            for i in range(4):
                bank = (OWNB, PARB)[h][i]
                mm(bank, "qw", "sw_", "qz%d" % h, "sz%d" % h, T.qw[:, 128 * i:128 * i + 128], T.sw_[:, 128 * i:128 * i + 128], T.qz[:, 160 * h:160 * h + 160], T.sz[:, 160 * h:160 * h + 160], 160)
                op("s", "act", ["ps%d" % bank], [("hh", i, h)], T.hh[:, C * i + 160 * h:C * i + 160 * h + 160], T["ps%d" % bank][:, 0:160], F.Copy, scale=2.0 ** -6)
        if r < 2:
            op("v", "tt", ["dd", "sg"], ["dd"], T.dd[:], T.dd[:], T.sg[:], A.add)
        for i in range(4):
            op("v", "tt", [("hh", i, 0), ("hh", i, 1), ("tu", i), "ep%d" % r], [("xt", i)], T.xt[:, i::4],
               T.hh[:, C * i:C * i + C].indirect(li("ep%d" % r)), T.tu[:, C * i:C * i + C], A.add)
        n = r + 1
        op("v", "quant", [("xt", i) for i in range(4)], ["qx%d" % n, "sx%d" % n], T["qx%d" % n][:], T["sx%d" % n][:], T.xt[:])

    dma("y", "doc", ["qx3"], [], T.oc[:], T.qx3[:].bitcast(dt.uint8))
    for k in range(4):
        dma("s" if k < 2 else "y", "ds%d" % k, ["sx3"], [], T.osc[4 * k:4 * k + 4, :], T.sx3[32 * k:32 * k + 4, :])
    mm(0, "qv_", "sv", "qx3", "sx3", T.qv_[:], T.sv[:], T.qx3[:], T.sx3[:], C)
    op("v", "copy", ["ps0"], ["ys"], T.ys[:], T.ps0[:, 0:C])
    dma("y", "dy0", ["ys"], [], T.y[:], T.ys[:])
    for s, n in total.items():
        g.wait_ge(T.sem[s], n)
